import numpy as np
import ml_dtypes


def mxq(x, axis, fmt="e4m3"):
    dtype, down = {"e4m3": (ml_dtypes.float8_e4m3fn, 7), "e5m2": (ml_dtypes.float8_e5m2, 14)}[fmt]
    v = np.moveaxis(np.asarray(x, np.float32).astype(ml_dtypes.bfloat16).astype(np.float64), axis, -1)
    blocks = v.reshape(v.shape[:-1] + (-1, 32))
    amax = np.abs(blocks).max(-1, keepdims=True)
    byte = np.maximum(np.where(amax > 0, np.frexp(amax)[1] - 1 + 127, 0) - down, 1)
    scale = np.exp2(byte - 127.0)
    codes = (blocks / scale).astype(np.float32).astype(dtype).astype(np.float64)
    return np.moveaxis((codes * scale).reshape(v.shape), -1, axis)


WIDE = False


def mx_kscale(k):
    if not WIDE:
        return np.ones(k)
    levels = np.array([10, -10, 5, -5, 0])
    if k % 512:
        return np.exp2(np.random.permutation(np.resize(levels, k // 32))).repeat(32)
    a = np.empty((k // 512, 16))
    for p in range(k // 512):
        a[p, :8] = np.random.permutation(np.resize(levels, 8))
        for g in range(8):
            far = levels[np.abs(levels - a[p, g]) >= 10]
            a[p, g + 8] = far[np.random.randint(len(far))]
    return np.exp2(a.ravel()).repeat(32)


def f64(x):
    return np.asarray(x).astype(np.float64)


def striped8(idx):
    return np.asarray(idx).reshape(8, -1, 16).transpose(0, 2, 1).reshape(128, -1).astype(np.uint16)


def unstriped8(offs):
    return offs.reshape(8, 16, -1).transpose(0, 2, 1).reshape(8, -1).astype(np.int64)


def pick8(x, idx, run):
    r = np.arange(len(x))
    return x[r[:, None], idx[r % (8 * run) // run]]


E2M1 = np.array([0.0, 0.5, 1.0, 1.5, 2.0, 3.0, 4.0, 6.0, -0.0, -0.5, -1.0, -1.5, -2.0, -3.0, -4.0, -6.0])


def pack_weight(w, fmt):
    k, n = w.shape
    w = f64(np.asarray(w, np.float32).astype(ml_dtypes.bfloat16)).reshape(k // 32, 32, n)
    amax = np.abs(w).max(1)
    if fmt == "e4m3":
        byte = np.frexp(amax)[1] - 1 + 127 - 7
    else:
        mant, ex = np.frexp(amax / 6.0)
        byte = np.where(mant > 0.5, ex, ex - 1) + 127
    byte = np.clip(np.where(amax > 0, byte, 1), 1, 254)
    scaled = (w * np.exp2(127.0 - byte)[:, None, :]).reshape(k, n).astype(np.float32)
    by_word = np.ascontiguousarray(scaled.reshape(k // 512, 128, 4, n).transpose(0, 1, 3, 2))
    if fmt == "e4m3":
        words = by_word.astype(ml_dtypes.float8_e4m3fn).view(np.uint8)
    else:
        c = by_word.astype(ml_dtypes.float4_e2m1fn).view(np.uint8) & 0xF
        words = (c[..., 0::2] | (c[..., 1::2] << 4)).reshape(k // 512, 128, 2 * n)
    return np.ascontiguousarray(words), np.ascontiguousarray(byte.astype(np.uint8).reshape(k // 512, 16, n))


def unpack_weight(words, scales, fmt):
    g, _, n = scales.shape
    words = np.ascontiguousarray(words).reshape(g, 128, n, -1)
    if fmt == "e4m3":
        vals = words.view(ml_dtypes.float8_e4m3fn).astype(np.float64)
    else:
        nib = np.empty((g, 128, n, 4), np.uint8)
        nib[..., 0::2] = words & 0xF
        nib[..., 1::2] = words >> 4
        vals = E2M1[nib]
    vals = vals * np.repeat(np.exp2(scales.astype(np.float64) - 127.0), 8, axis=1)[..., None]
    return vals.transpose(0, 1, 3, 2).reshape(g * 512, n)


D, V, Q, I = 1024, 2048, 128, 512


def setup_inputs():
    n = np.random.standard_normal
    idx = np.stack([np.random.permutation(V)[:I] for _ in range(8)])
    fd = mx_kscale(D)
    vocp = pack_weight(n((D, V)) / fd[:, None], "e2m1")
    return {
        "hid": (n((D, Q)) * 1.0 / np.sqrt(D) * fd[:, None]).astype(np.float32),
        "voc_words": vocp[0],
        "voc_scales": vocp[1],
        "bonus": (0.5 * n((Q, I))).astype(np.float32),
        "offs": striped8(idx),
    }


def reference(hid, voc_words, voc_scales, bonus, offs):
    idx = unstriped8(offs)
    vocu = unpack_weight(voc_words, voc_scales, "e2m1")
    hidq = mxq(f64(hid), 0, "e4m3")
    a = hidq.T @ vocu
    s = pick8(a, idx, 16) + f64(bonus)
    p = np.exp(s - np.max(s, axis=1, keepdims=True))
    w = p / np.sum(p, axis=1, keepdims=True) * 512.0
    y = np.zeros((Q, V))
    y[np.arange(Q)[:, None], idx[np.arange(Q) % 128 // 16]] = w
    return y

@@ -1,0 +1,124 @@
+from contextlib import ExitStack
+
+import concourse.mybir as mybir
+
+D, V, Q, I = 1024, 2048, 128, 512
+FLOPS = 2 * D * V * Q
+
+F32 = mybir.dt.float32
+BF16 = mybir.dt.bfloat16
+I32 = mybir.dt.int32
+U32 = mybir.dt.uint32
+U16 = mybir.dt.uint16
+U8 = mybir.dt.uint8
+FP8X4 = mybir.dt.float8_e4m3fn_x4
+FP4X4 = mybir.dt.float4_e2m1fn_x4
+ALU = mybir.AluOpType
+ACT = mybir.ActivationFunctionType
+AX = mybir.AxisListType
+
+P = 128
+PACK = 4
+K_PASS = P * PACK
+PASSES = D // K_PASS
+BANK = 512
+HALF = V // 2
+
+
+def tile_attend_beamvocab_kernel(tc, hid, voc_words, voc_scales, bonus, offs, out):
+    nc = tc.nc
+    with ExitStack() as ctx:
+        keep = ctx.enter_context(tc.tile_pool(name="keep", bufs=1))
+        psum = ctx.enter_context(tc.psum_pool(name="psum", bufs=1))
+
+        offsets = keep.tile([P, I // 16], U16, name="offsets")
+        planes = keep.tile([P, PASSES * V], U8, name="planes", align_bytes=64)
+        nc.vector.memset(planes[:, : 3 * V // 2].bitcast(I32), 0)
+        nc.gpsimd.memset(planes[:, 3 * V // 2 :].bitcast(I32), 0)
+
+        warm = keep.tile([P, 8], F32, name="warm")
+        warm2 = keep.tile([P, 8], F32, name="warm2")
+        nc.gpsimd.memset(warm[:], 0.0)
+
+        raw = [keep.tile([P, PACK, Q], F32, name="raw%d" % z) for z in range(PASSES)]
+        words = [[keep.tile([P, 2 * HALF], U8, name="words%d_%d" % (z, h), align_bytes=64) for h in range(2)] for z in range(PASSES)]
+
+        def load_hid(z):
+            nc.sync.dma_start(raw[z][:], hid[z * K_PASS : (z + 1) * K_PASS, :].rearrange("(p t) q -> p t q", t=PACK))
+
+        def load_words(z, h):
+            nc.sync.dma_start(words[z][h][:].bitcast(I32), voc_words[z, :, h * 2 * HALF : (h + 1) * 2 * HALF].bitcast(I32))
+
+        load_hid(0)
+        planes3 = planes[:].bitcast(I32).rearrange("p (z c) -> p z c", z=PASSES)
+        scales3 = voc_scales.bitcast(I32).rearrange("z (a r) c -> r a z c", r=4)
+        load_words(0, 0)
+        for r in range(4):
+            nc.sync.dma_start(planes3[r:P:32, :, :], scales3[r])
+        nc.scalar.activation(warm2[:], warm[:], ACT.Exp)
+        load_hid(1)
+        load_words(0, 1)
+        load_words(1, 0)
+        load_words(1, 1)
+        extra = keep.tile([P, I], F32, name="extra")
+        nc.sync.dma_start(extra[:], bonus)
+        nc.sync.dma_start(offsets[:], offs)
+
+        spread = keep.tile([P, V], F32, name="spread")
+        nc.vector.memset(spread[:], 0.0)
+
+        codes = []
+        hscales = []
+        for z in range(PASSES):
+            grouped = keep.tile([P, Q, PACK], BF16, name="grouped%d" % z, align_bytes=64)
+            nc.vector.tensor_copy(
+                grouped[:].rearrange("p (c i) t -> p c t i", i=4),
+                raw[z][:].rearrange("p t (c i) -> p c t i", i=4),
+            )
+            code = keep.tile([P, Q], U32, name="code%d" % z, align_bytes=64)
+            hscale = keep.tile([P, Q], U8, name="hscale%d" % z, align_bytes=64)
+            nc.vector.quantize_mx(code[:].bitcast(FP8X4), hscale[:], grouped[:].rearrange("p q t -> p (q t)"))
+            codes.append(code)
+            hscales.append(hscale)
+
+        logits = keep.tile([P, V], F32, name="logits")
+
+        def one_pass(acc, z, c0, n):
+            h, c = divmod(c0, HALF)
+            nc.tensor.matmul_mx(
+                acc[:],
+                lhsT=codes[z][:].bitcast(FP8X4),
+                lhsT_scale=hscales[z][:],
+                rhs=words[z][h][:, 2 * c : 2 * (c + n)].bitcast(FP4X4),
+                rhs_scale=planes[:, z * V + c0 : z * V + c0 + n],
+                start=(z == 0),
+                stop=(z == PASSES - 1),
+            )
+
+        copiers = (nc.scalar.copy, nc.vector.tensor_copy)
+        banks = [psum.tile([P, BANK], F32, name="bank%d" % b) for b in range(3)]
+        for z in range(PASSES):
+            for b in range(3):
+                one_pass(banks[b], z, b * BANK, BANK)
+        for b in range(3):
+            copiers[b % 2](logits[:, b * BANK : (b + 1) * BANK], banks[b][:])
+        for j in range(4):
+            c0 = 3 * BANK + j * P
+            narrow = psum.tile([P, P], F32, name="narrow%d" % j)
+            for z in range(PASSES):
+                one_pass(narrow, z, c0, P)
+            copiers[(j + 1) % 2](logits[:, c0 : c0 + P], narrow[:])
+
+        s = keep.tile([P, I], F32, name="s")
+        nc.vector.tensor_tensor(s[:], logits[:].indirect(offsets[:]), extra[:], ALU.add)
+        negmax = keep.tile([P, 1], F32, name="negmax")
+        nc.vector.tensor_reduce(negmax[:], s[:], AX.X, ALU.max, negate=True)
+        p = keep.tile([P, I], F32, name="p")
+        total = keep.tile([P, 1], F32, name="total")
+        nc.scalar.activation(p[:], s[:], ACT.Exp, bias=negmax[:], accum_out=total[:])
+        inv = keep.tile([P, 1], F32, name="inv")
+        nc.vector.reciprocal(inv[:], total[:])
+        w = keep.tile([P, I], F32, name="w")
+        nc.vector.tensor_scalar(w[:], p[:], inv[:], float(I), ALU.mult, ALU.mult)
+        nc.vector.tensor_copy(spread[:].indirect(offsets[:]), w[:])
+        nc.sync.dma_start(out, spread[:])

@@ -23,6 +23,7 @@ K_PASS = P * PACK
 PASSES = D // K_PASS
 BANK = 512
 HALF = V // 2
+WARM = 8
 
 
 def tile_attend_beamvocab_kernel(tc, hid, voc_words, voc_scales, bonus, offs, out):
@@ -33,44 +34,48 @@ def tile_attend_beamvocab_kernel(tc, hid, voc_words, voc_scales, bonus, offs, ou
 
         offsets = keep.tile([P, I // 16], U16, name="offsets")
         planes = keep.tile([P, PASSES * V], U8, name="planes", align_bytes=64)
-        nc.vector.memset(planes[:, : 3 * V // 2].bitcast(I32), 0)
-        nc.gpsimd.memset(planes[:, 3 * V // 2 :].bitcast(I32), 0)
+        nc.vector.memset(planes[:].bitcast(I32), 0)
 
         warm = keep.tile([P, 8], F32, name="warm")
         warm2 = keep.tile([P, 8], F32, name="warm2")
         nc.gpsimd.memset(warm[:], 0.0)
 
         raw = [keep.tile([P, PACK, Q], F32, name="raw%d" % z) for z in range(PASSES)]
-        words = [[keep.tile([P, 2 * HALF], U8, name="words%d_%d" % (z, h), align_bytes=64) for h in range(2)] for z in range(PASSES)]
+        front = [keep.tile([P, 2 * HALF], U8, name="front%d" % z, align_bytes=64) for z in range(PASSES)]
+        back = [keep.tile([P, PASSES * 2 * BANK], U8, name="back%d" % j, align_bytes=64) for j in range(2)]
 
         def load_hid(z):
             nc.sync.dma_start(raw[z][:], hid[z * K_PASS : (z + 1) * K_PASS, :].rearrange("(p t) q -> p t q", t=PACK))
 
-        def load_words(z, h):
-            nc.sync.dma_start(words[z][h][:].bitcast(I32), voc_words[z, :, h * 2 * HALF : (h + 1) * 2 * HALF].bitcast(I32))
+        def load_front(z):
+            nc.sync.dma_start(front[z][:].bitcast(I32), voc_words[z, :, : 2 * HALF].bitcast(I32))
+
+        def load_back(j):
+            lo = 2 * (HALF + j * BANK)
+            nc.sync.dma_start(
+                back[j][:].bitcast(I32).rearrange("p (z c) -> p z c", z=PASSES),
+                voc_words[:, :, lo : lo + 2 * BANK].bitcast(I32).rearrange("z p c -> p z c"),
+            )
 
         load_hid(0)
+        load_front(0)
+        load_hid(1)
         planes3 = planes[:].bitcast(I32).rearrange("p (z c) -> p z c", z=PASSES)
         scales3 = voc_scales.bitcast(I32).rearrange("z (a r) c -> r a z c", r=4)
-        load_words(0, 0)
         for r in range(4):
             nc.sync.dma_start(planes3[r:P:32, :, :], scales3[r])
         nc.scalar.activation(warm2[:], warm[:], ACT.Exp)
-        load_hid(1)
-        load_words(0, 1)
-        load_words(1, 0)
-        load_words(1, 1)
+        load_front(1)
+        load_back(0)
+        load_back(1)
         extra = keep.tile([P, I], F32, name="extra")
         nc.sync.dma_start(extra[:], bonus)
         nc.sync.dma_start(offsets[:], offs)
 
-        spread = keep.tile([P, V], F32, name="spread")
-        nc.vector.memset(spread[:], 0.0)
-
         codes = []
         hscales = []
         for z in range(PASSES):
-            grouped = keep.tile([P, Q, PACK], BF16, name="grouped%d" % z, align_bytes=64)
+            grouped = keep.tile([P, Q, PACK], BF16, name="grouped%d" % z, tag="grouped%d" % z, align_bytes=64)
             nc.vector.tensor_copy(
                 grouped[:].rearrange("p (c i) t -> p c t i", i=4),
                 raw[z][:].rearrange("p t (c i) -> p c t i", i=4),
@@ -81,25 +86,45 @@ def tile_attend_beamvocab_kernel(tc, hid, voc_words, voc_scales, bonus, offs, ou
             codes.append(code)
             hscales.append(hscale)
 
+        spread = keep.tile([P, V], F32, name="spread", tag="grouped1", align_bytes=64)
+        nc.vector.memset(spread[:], 0.0)
+
         logits = keep.tile([P, V], F32, name="logits")
 
         def one_pass(acc, z, c0, n):
-            h, c = divmod(c0, HALF)
+            if c0 < HALF:
+                moving = front[z][:, 2 * c0 : 2 * (c0 + n)]
+            else:
+                j, c = divmod(c0 - HALF, BANK)
+                moving = back[j][:, 2 * (z * BANK + c) : 2 * (z * BANK + c + n)]
             nc.tensor.matmul_mx(
                 acc[:],
                 lhsT=codes[z][:].bitcast(FP8X4),
                 lhsT_scale=hscales[z][:],
-                rhs=words[z][h][:, 2 * c : 2 * (c + n)].bitcast(FP4X4),
+                rhs=moving.bitcast(FP4X4),
                 rhs_scale=planes[:, z * V + c0 : z * V + c0 + n],
                 start=(z == 0),
                 stop=(z == PASSES - 1),
             )
 
+        idle = psum.tile([P, P], F32, name="idle")
+        for j in range(WARM):
+            nc.tensor.matmul_mx(
+                idle[:],
+                lhsT=codes[0][:].bitcast(FP8X4),
+                lhsT_scale=hscales[0][:],
+                rhs=front[0][:, 2 * j * P : 2 * (j + 1) * P].bitcast(FP4X4),
+                rhs_scale=hscales[0][:],
+                start=(j == 0),
+                stop=(j == WARM - 1),
+            )
+
         copiers = (nc.scalar.copy, nc.vector.tensor_copy)
         banks = [psum.tile([P, BANK], F32, name="bank%d" % b) for b in range(3)]
-        for z in range(PASSES):
-            for b in range(3):
-                one_pass(banks[b], z, b * BANK, BANK)
+        for group in ((0, 1), (2,)):
+            for z in range(PASSES):
+                for b in group:
+                    one_pass(banks[b], z, b * BANK, BANK)
         for b in range(3):
             copiers[b % 2](logits[:, b * BANK : (b + 1) * BANK], banks[b][:])
         for j in range(4):

@@ -36,10 +36,6 @@ def tile_attend_beamvocab_kernel(tc, hid, voc_words, voc_scales, bonus, offs, ou
         planes = keep.tile([P, PASSES * V], U8, name="planes", align_bytes=64)
         nc.vector.memset(planes[:].bitcast(I32), 0)
 
-        warm = keep.tile([P, 8], F32, name="warm")
-        warm2 = keep.tile([P, 8], F32, name="warm2")
-        nc.gpsimd.memset(warm[:], 0.0)
-
         raw = [keep.tile([P, PACK, Q], F32, name="raw%d" % z) for z in range(PASSES)]
         front = [keep.tile([P, 2 * HALF], U8, name="front%d" % z, align_bytes=64) for z in range(PASSES)]
         back = [keep.tile([P, PASSES * 2 * BANK], U8, name="back%d" % j, align_bytes=64) for j in range(2)]
@@ -64,7 +60,6 @@ def tile_attend_beamvocab_kernel(tc, hid, voc_words, voc_scales, bonus, offs, ou
         scales3 = voc_scales.bitcast(I32).rearrange("z (a r) c -> r a z c", r=4)
         for r in range(4):
             nc.sync.dma_start(planes3[r:P:32, :, :], scales3[r])
-        nc.scalar.activation(warm2[:], warm[:], ACT.Exp)
         load_front(1)
         load_back(0)
         load_back(1)
@@ -119,7 +114,10 @@ def tile_attend_beamvocab_kernel(tc, hid, voc_words, voc_scales, bonus, offs, ou
                 stop=(j == WARM - 1),
             )
 
-        copiers = (nc.scalar.copy, nc.vector.tensor_copy)
+        def scalar_copy(dst, src):
+            nc.scalar.activation(dst, src, ACT.Copy)
+
+        copiers = (scalar_copy, nc.vector.tensor_copy)
         banks = [psum.tile([P, BANK], F32, name="bank%d" % b) for b in range(3)]
         for group in ((0, 1), (2,)):
             for z in range(PASSES):
@@ -146,4 +144,5 @@ def tile_attend_beamvocab_kernel(tc, hid, voc_words, voc_scales, bonus, offs, ou
         w = keep.tile([P, I], F32, name="w")
         nc.vector.tensor_scalar(w[:], p[:], inv[:], float(I), ALU.mult, ALU.mult)
         nc.vector.tensor_copy(spread[:].indirect(offsets[:]), w[:])
-        nc.sync.dma_start(out, spread[:])
+        nc.sync.dma_start(out[:, :HALF], spread[:, :HALF])
+        nc.scalar.dma_start(out[:, HALF:], spread[:, HALF:])

@@ -21,9 +21,13 @@ P = 128
 PACK = 4
 K_PASS = P * PACK
 PASSES = D // K_PASS
+WORD_BYTES = 2
+SCALE_ROWS = 4
 BANK = 512
-HALF = V // 2
-WARM = 8
+NARROW = 128
+WORD_PIECES = (((0, 512), (512, 1024), (1024, 2048)), ((0, 1024), (1024, 2048)))
+VECTOR_ZEROED = 3 * PASSES * V // 4
+WARM_PASSES = PASSES * V // 4 // NARROW
 
 
 def tile_attend_beamvocab_kernel(tc, hid, voc_words, voc_scales, bonus, offs, out):
@@ -32,117 +36,109 @@ def tile_attend_beamvocab_kernel(tc, hid, voc_words, voc_scales, bonus, offs, ou
         keep = ctx.enter_context(tc.tile_pool(name="keep", bufs=1))
         psum = ctx.enter_context(tc.psum_pool(name="psum", bufs=1))
 
-        offsets = keep.tile([P, I // 16], U16, name="offsets")
-        planes = keep.tile([P, PASSES * V], U8, name="planes", align_bytes=64)
-        nc.vector.memset(planes[:].bitcast(I32), 0)
+        voc_planes = keep.tile([P, PASSES * V], U8, name="voc_planes", align_bytes=64)
+        nc.vector.memset(voc_planes[:, :VECTOR_ZEROED].bitcast(I32), 0)
+        nc.gpsimd.memset(voc_planes[:, VECTOR_ZEROED:].bitcast(I32), 0)
 
-        raw = [keep.tile([P, PACK, Q], F32, name="raw%d" % z) for z in range(PASSES)]
-        front = [keep.tile([P, 2 * HALF], U8, name="front%d" % z, align_bytes=64) for z in range(PASSES)]
-        back = [keep.tile([P, PASSES * 2 * BANK], U8, name="back%d" % j, align_bytes=64) for j in range(2)]
+        hid_rows = {}
+        word_tiles = {}
 
         def load_hid(z):
-            nc.sync.dma_start(raw[z][:], hid[z * K_PASS : (z + 1) * K_PASS, :].rearrange("(p t) q -> p t q", t=PACK))
+            hid_rows[z] = keep.tile([P, PACK, Q], F32, name="hid_rows%d" % z)
+            rows = hid[z * K_PASS : (z + 1) * K_PASS, :]
+            nc.sync.dma_start(hid_rows[z][:], rows.rearrange("(p t) q -> p t q", t=PACK))
 
-        def load_front(z):
-            nc.sync.dma_start(front[z][:].bitcast(I32), voc_words[z, :, : 2 * HALF].bitcast(I32))
+        def load_words(z, piece):
+            lo, hi = WORD_PIECES[z][piece]
+            tile = keep.tile([P, WORD_BYTES * (hi - lo)], U8, name="words%d_%d" % (z, piece), align_bytes=64)
+            nc.sync.dma_start(tile[:].bitcast(I32), voc_words[z, :, WORD_BYTES * lo : WORD_BYTES * hi].bitcast(I32))
+            word_tiles[z, piece] = tile
 
-        def load_back(j):
-            lo = 2 * (HALF + j * BANK)
-            nc.sync.dma_start(
-                back[j][:].bitcast(I32).rearrange("p (z c) -> p z c", z=PASSES),
-                voc_words[:, :, lo : lo + 2 * BANK].bitcast(I32).rearrange("z p c -> p z c"),
-            )
+        def words_of(z, c0, n):
+            piece = max(k for k, (lo, hi) in enumerate(WORD_PIECES[z]) if lo <= c0)
+            at = c0 - WORD_PIECES[z][piece][0]
+            return word_tiles[z, piece][:, WORD_BYTES * at : WORD_BYTES * (at + n)].bitcast(FP4X4)
 
         load_hid(0)
-        load_front(0)
+        load_words(0, 0)
+        planes_by_pass = voc_planes[:].bitcast(I32).rearrange("p (z c) -> p z c", z=PASSES)
+        scale_rows = voc_scales.bitcast(I32).rearrange("z (a r) c -> r a z c", r=SCALE_ROWS)
+        for r in range(SCALE_ROWS):
+            nc.sync.dma_start(planes_by_pass[r:P:32, :, :], scale_rows[r])
+        load_words(0, 1)
         load_hid(1)
-        planes3 = planes[:].bitcast(I32).rearrange("p (z c) -> p z c", z=PASSES)
-        scales3 = voc_scales.bitcast(I32).rearrange("z (a r) c -> r a z c", r=4)
-        for r in range(4):
-            nc.sync.dma_start(planes3[r:P:32, :, :], scales3[r])
-        load_front(1)
-        load_back(0)
-        load_back(1)
-        extra = keep.tile([P, I], F32, name="extra")
-        nc.sync.dma_start(extra[:], bonus)
+        load_words(0, 2)
+        load_words(1, 0)
+        load_words(1, 1)
+        bonus_sb = keep.tile([P, I], F32, name="bonus_sb")
+        nc.sync.dma_start(bonus_sb[:], bonus)
+        offsets = keep.tile([P, I // 16], U16, name="offsets")
         nc.sync.dma_start(offsets[:], offs)
 
-        codes = []
-        hscales = []
+        hid_codes = []
+        hid_planes = []
         for z in range(PASSES):
             grouped = keep.tile([P, Q, PACK], BF16, name="grouped%d" % z, tag="grouped%d" % z, align_bytes=64)
             nc.vector.tensor_copy(
                 grouped[:].rearrange("p (c i) t -> p c t i", i=4),
-                raw[z][:].rearrange("p t (c i) -> p c t i", i=4),
+                hid_rows[z][:].rearrange("p t (c i) -> p c t i", i=4),
             )
-            code = keep.tile([P, Q], U32, name="code%d" % z, align_bytes=64)
-            hscale = keep.tile([P, Q], U8, name="hscale%d" % z, align_bytes=64)
-            nc.vector.quantize_mx(code[:].bitcast(FP8X4), hscale[:], grouped[:].rearrange("p q t -> p (q t)"))
-            codes.append(code)
-            hscales.append(hscale)
+            codes = keep.tile([P, Q], U32, name="hid_codes%d" % z, align_bytes=64)
+            plane = keep.tile([P, Q], U8, name="hid_plane%d" % z, align_bytes=64)
+            nc.vector.quantize_mx(codes[:].bitcast(FP8X4), plane[:], grouped[:].rearrange("p q t -> p (q t)"))
+            hid_codes.append(codes)
+            hid_planes.append(plane)
 
-        spread = keep.tile([P, V], F32, name="spread", tag="grouped1", align_bytes=64)
+        spread = keep.tile([P, V], F32, name="spread", tag="grouped0", align_bytes=64)
         nc.vector.memset(spread[:], 0.0)
 
-        logits = keep.tile([P, V], F32, name="logits")
-
-        def one_pass(acc, z, c0, n):
-            if c0 < HALF:
-                moving = front[z][:, 2 * c0 : 2 * (c0 + n)]
-            else:
-                j, c = divmod(c0 - HALF, BANK)
-                moving = back[j][:, 2 * (z * BANK + c) : 2 * (z * BANK + c + n)]
+        unused = psum.tile([P, NARROW], F32, name="unused")
+        for j in range(WARM_PASSES):
             nc.tensor.matmul_mx(
-                acc[:],
-                lhsT=codes[z][:].bitcast(FP8X4),
-                lhsT_scale=hscales[z][:],
-                rhs=moving.bitcast(FP4X4),
-                rhs_scale=planes[:, z * V + c0 : z * V + c0 + n],
-                start=(z == 0),
-                stop=(z == PASSES - 1),
-            )
-
-        idle = psum.tile([P, P], F32, name="idle")
-        for j in range(WARM):
-            nc.tensor.matmul_mx(
-                idle[:],
-                lhsT=codes[0][:].bitcast(FP8X4),
-                lhsT_scale=hscales[0][:],
-                rhs=front[0][:, 2 * j * P : 2 * (j + 1) * P].bitcast(FP4X4),
-                rhs_scale=hscales[0][:],
+                unused[:],
+                lhsT=hid_codes[0][:].bitcast(FP8X4),
+                lhsT_scale=hid_planes[0][:],
+                rhs=words_of(0, 0, NARROW),
+                rhs_scale=hid_planes[0][:],
                 start=(j == 0),
-                stop=(j == WARM - 1),
+                stop=(j == WARM_PASSES - 1),
             )
 
-        def scalar_copy(dst, src):
-            nc.scalar.activation(dst, src, ACT.Copy)
+        groups = [(c0, BANK) for c0 in range(0, V - BANK, BANK)]
+        groups = groups + [(c0, NARROW) for c0 in range(V - BANK, V, NARROW)]
+        sums = [psum.tile([P, n], F32, name="sums%d" % c0) for c0, n in groups]
+        for z in range(PASSES):
+            for (c0, n), acc in zip(groups, sums):
+                nc.tensor.matmul_mx(
+                    acc[:],
+                    lhsT=hid_codes[z][:].bitcast(FP8X4),
+                    lhsT_scale=hid_planes[z][:],
+                    rhs=words_of(z, c0, n),
+                    rhs_scale=voc_planes[:, z * V + c0 : z * V + c0 + n],
+                    start=(z == 0),
+                    stop=(z == PASSES - 1),
+                )
 
-        copiers = (scalar_copy, nc.vector.tensor_copy)
-        banks = [psum.tile([P, BANK], F32, name="bank%d" % b) for b in range(3)]
-        for group in ((0, 1), (2,)):
-            for z in range(PASSES):
-                for b in group:
-                    one_pass(banks[b], z, b * BANK, BANK)
-        for b in range(3):
-            copiers[b % 2](logits[:, b * BANK : (b + 1) * BANK], banks[b][:])
-        for j in range(4):
-            c0 = 3 * BANK + j * P
-            narrow = psum.tile([P, P], F32, name="narrow%d" % j)
-            for z in range(PASSES):
-                one_pass(narrow, z, c0, P)
-            copiers[(j + 1) % 2](logits[:, c0 : c0 + P], narrow[:])
+        on_scalar = (0, 2, len(groups) - 1)
+        logits = keep.tile([P, V], F32, name="logits")
+        for g, ((c0, n), acc) in enumerate(zip(groups, sums)):
+            if g in on_scalar:
+                nc.scalar.activation(logits[:, c0 : c0 + n], acc[:], ACT.Copy)
+            else:
+                nc.vector.tensor_copy(logits[:, c0 : c0 + n], acc[:])
 
-        s = keep.tile([P, I], F32, name="s")
-        nc.vector.tensor_tensor(s[:], logits[:].indirect(offsets[:]), extra[:], ALU.add)
-        negmax = keep.tile([P, 1], F32, name="negmax")
-        nc.vector.tensor_reduce(negmax[:], s[:], AX.X, ALU.max, negate=True)
-        p = keep.tile([P, I], F32, name="p")
+        scores = keep.tile([P, I], F32, name="scores")
+        nc.vector.tensor_tensor(scores[:], logits[:].indirect(offsets[:]), bonus_sb[:], ALU.add)
+
+        neg_max = keep.tile([P, 1], F32, name="neg_max")
+        nc.vector.tensor_reduce(neg_max[:], scores[:], AX.X, ALU.max, negate=True)
+        exps = keep.tile([P, I], F32, name="exps")
         total = keep.tile([P, 1], F32, name="total")
-        nc.scalar.activation(p[:], s[:], ACT.Exp, bias=negmax[:], accum_out=total[:])
-        inv = keep.tile([P, 1], F32, name="inv")
-        nc.vector.reciprocal(inv[:], total[:])
-        w = keep.tile([P, I], F32, name="w")
-        nc.vector.tensor_scalar(w[:], p[:], inv[:], float(I), ALU.mult, ALU.mult)
-        nc.vector.tensor_copy(spread[:].indirect(offsets[:]), w[:])
-        nc.sync.dma_start(out[:, :HALF], spread[:, :HALF])
-        nc.scalar.dma_start(out[:, HALF:], spread[:, HALF:])
+        nc.scalar.activation(exps[:], scores[:], ACT.Exp, bias=neg_max[:], accum_out=total[:])
+
+        inv_total = keep.tile([P, 1], F32, name="inv_total")
+        nc.vector.reciprocal(inv_total[:], total[:])
+        weights = keep.tile([P, I], F32, name="weights")
+        nc.vector.tensor_scalar(weights[:], exps[:], inv_total[:], float(I), ALU.mult, ALU.mult)
+        nc.vector.tensor_copy(spread[:].indirect(offsets[:]), weights[:])
+        nc.sync.dma_start(out, spread[:])

@@ -25,9 +25,7 @@ WORD_BYTES = 2
 SCALE_ROWS = 4
 BANK = 512
 NARROW = 128
-WORD_PIECES = (((0, 512), (512, 1024), (1024, 2048)), ((0, 1024), (1024, 2048)))
-VECTOR_ZEROED = 3 * PASSES * V // 4
-WARM_PASSES = PASSES * V // 4 // NARROW
+WORD_PIECES = (((0, 1024), (1024, 2048)), ((0, 512), (512, 1024), (1024, 1536), (1536, 2048)))
 
 
 def tile_attend_beamvocab_kernel(tc, hid, voc_words, voc_scales, bonus, offs, out):
@@ -36,9 +34,11 @@ def tile_attend_beamvocab_kernel(tc, hid, voc_words, voc_scales, bonus, offs, ou
         keep = ctx.enter_context(tc.tile_pool(name="keep", bufs=1))
         psum = ctx.enter_context(tc.psum_pool(name="psum", bufs=1))
 
-        voc_planes = keep.tile([P, PASSES * V], U8, name="voc_planes", align_bytes=64)
-        nc.vector.memset(voc_planes[:, :VECTOR_ZEROED].bitcast(I32), 0)
-        nc.gpsimd.memset(voc_planes[:, VECTOR_ZEROED:].bitcast(I32), 0)
+        voc_planes = []
+        for z in range(PASSES):
+            voc_plane = keep.tile([P, V], U8, name="voc_plane%d" % z, align_bytes=64)
+            nc.vector.memset(voc_plane[:].bitcast(I32), 0)
+            voc_planes.append(voc_plane)
 
         hid_rows = {}
         word_tiles = {}
@@ -59,17 +59,19 @@ def tile_attend_beamvocab_kernel(tc, hid, voc_words, voc_scales, bonus, offs, ou
             at = c0 - WORD_PIECES[z][piece][0]
             return word_tiles[z, piece][:, WORD_BYTES * at : WORD_BYTES * (at + n)].bitcast(FP4X4)
 
+        def load_scales(z):
+            scale_rows = voc_scales[z].bitcast(I32).rearrange("(a r) c -> r a c", r=SCALE_ROWS)
+            for r in range(SCALE_ROWS):
+                nc.sync.dma_start(voc_planes[z][:].bitcast(I32)[r:P:32, :], scale_rows[r])
+
         load_hid(0)
         load_words(0, 0)
-        planes_by_pass = voc_planes[:].bitcast(I32).rearrange("p (z c) -> p z c", z=PASSES)
-        scale_rows = voc_scales.bitcast(I32).rearrange("z (a r) c -> r a z c", r=SCALE_ROWS)
-        for r in range(SCALE_ROWS):
-            nc.sync.dma_start(planes_by_pass[r:P:32, :, :], scale_rows[r])
-        load_words(0, 1)
+        load_scales(0)
         load_hid(1)
-        load_words(0, 2)
-        load_words(1, 0)
-        load_words(1, 1)
+        load_words(0, 1)
+        load_scales(1)
+        for piece in range(len(WORD_PIECES[1])):
+            load_words(1, piece)
         bonus_sb = keep.tile([P, I], F32, name="bonus_sb")
         nc.sync.dma_start(bonus_sb[:], bonus)
         offsets = keep.tile([P, I // 16], U16, name="offsets")
@@ -89,20 +91,8 @@ def tile_attend_beamvocab_kernel(tc, hid, voc_words, voc_scales, bonus, offs, ou
             hid_codes.append(codes)
             hid_planes.append(plane)
 
-        spread = keep.tile([P, V], F32, name="spread", tag="grouped0", align_bytes=64)
-        nc.vector.memset(spread[:], 0.0)
-
-        unused = psum.tile([P, NARROW], F32, name="unused")
-        for j in range(WARM_PASSES):
-            nc.tensor.matmul_mx(
-                unused[:],
-                lhsT=hid_codes[0][:].bitcast(FP8X4),
-                lhsT_scale=hid_planes[0][:],
-                rhs=words_of(0, 0, NARROW),
-                rhs_scale=hid_planes[0][:],
-                start=(j == 0),
-                stop=(j == WARM_PASSES - 1),
-            )
+        spread = keep.tile([P, V], F32, name="spread", tag="grouped1", align_bytes=64)
+        nc.gpsimd.memset(spread[:], 0.0)
 
         groups = [(c0, BANK) for c0 in range(0, V - BANK, BANK)]
         groups = groups + [(c0, NARROW) for c0 in range(V - BANK, V, NARROW)]
@@ -114,7 +104,7 @@ def tile_attend_beamvocab_kernel(tc, hid, voc_words, voc_scales, bonus, offs, ou
                     lhsT=hid_codes[z][:].bitcast(FP8X4),
                     lhsT_scale=hid_planes[z][:],
                     rhs=words_of(z, c0, n),
-                    rhs_scale=voc_planes[:, z * V + c0 : z * V + c0 + n],
+                    rhs_scale=voc_planes[z][:, c0 : c0 + n],
                     start=(z == 0),
                     stop=(z == PASSES - 1),
                 )

@@ -91,8 +91,8 @@ def tile_attend_beamvocab_kernel(tc, hid, voc_words, voc_scales, bonus, offs, ou
             hid_codes.append(codes)
             hid_planes.append(plane)
 
-        spread = keep.tile([P, V], F32, name="spread", tag="grouped1", align_bytes=64)
-        nc.gpsimd.memset(spread[:], 0.0)
+        spread = keep.tile([P, V], F32, name="spread", tag="grouped0", align_bytes=64)
+        nc.vector.memset(spread[:], 0.0)
 
         groups = [(c0, BANK) for c0 in range(0, V - BANK, BANK)]
         groups = groups + [(c0, NARROW) for c0 in range(V - BANK, V, NARROW)]

@@ -25,7 +25,7 @@ WORD_BYTES = 2
 SCALE_ROWS = 4
 BANK = 512
 NARROW = 128
-WORD_PIECES = (((0, 1024), (1024, 2048)), ((0, 512), (512, 1024), (1024, 1536), (1536, 2048)))
+WORD_PIECES = (((0, 512), (512, 1024), (1024, 2048)), ((0, 1024), (1024, 1536), (1536, 2048)))
 
 
 def tile_attend_beamvocab_kernel(tc, hid, voc_words, voc_scales, bonus, offs, out):
@@ -67,18 +67,22 @@ def tile_attend_beamvocab_kernel(tc, hid, voc_words, voc_scales, bonus, offs, ou
         load_hid(0)
         load_words(0, 0)
         load_scales(0)
-        load_hid(1)
         load_words(0, 1)
+        load_hid(1)
+        load_words(0, 2)
         load_scales(1)
         for piece in range(len(WORD_PIECES[1])):
             load_words(1, piece)
-        bonus_sb = keep.tile([P, I], F32, name="bonus_sb")
-        nc.sync.dma_start(bonus_sb[:], bonus)
         offsets = keep.tile([P, I // 16], U16, name="offsets")
         nc.sync.dma_start(offsets[:], offs)
+        bonus_sb = keep.tile([P, I], F32, name="bonus_sb")
+        nc.sync.dma_start(bonus_sb[:], bonus)
+
+        hid_planes = [keep.tile([P, Q + BANK * (1 - z)], U8, name="hid_plane%d" % z, align_bytes=64) for z in range(PASSES)]
+        zeros = hid_planes[0][:, Q:]
+        nc.vector.memset(zeros.bitcast(I32), 0)
 
         hid_codes = []
-        hid_planes = []
         for z in range(PASSES):
             grouped = keep.tile([P, Q, PACK], BF16, name="grouped%d" % z, tag="grouped%d" % z, align_bytes=64)
             nc.vector.tensor_copy(
@@ -86,10 +90,8 @@ def tile_attend_beamvocab_kernel(tc, hid, voc_words, voc_scales, bonus, offs, ou
                 hid_rows[z][:].rearrange("p t (c i) -> p c t i", i=4),
             )
             codes = keep.tile([P, Q], U32, name="hid_codes%d" % z, align_bytes=64)
-            plane = keep.tile([P, Q], U8, name="hid_plane%d" % z, align_bytes=64)
-            nc.vector.quantize_mx(codes[:].bitcast(FP8X4), plane[:], grouped[:].rearrange("p q t -> p (q t)"))
+            nc.vector.quantize_mx(codes[:].bitcast(FP8X4), hid_planes[z][:, :Q], grouped[:].rearrange("p q t -> p (q t)"))
             hid_codes.append(codes)
-            hid_planes.append(plane)
 
         spread = keep.tile([P, V], F32, name="spread", tag="grouped0", align_bytes=64)
         nc.vector.memset(spread[:], 0.0)
@@ -97,12 +99,22 @@ def tile_attend_beamvocab_kernel(tc, hid, voc_words, voc_scales, bonus, offs, ou
         groups = [(c0, BANK) for c0 in range(0, V - BANK, BANK)]
         groups = groups + [(c0, NARROW) for c0 in range(V - BANK, V, NARROW)]
         sums = [psum.tile([P, n], F32, name="sums%d" % c0) for c0, n in groups]
+
+        nc.tensor.matmul_mx(
+            sums[0][:],
+            lhsT=zeros.bitcast(FP8X4),
+            lhsT_scale=zeros[:, :Q],
+            rhs=words_of(0, 0, BANK),
+            rhs_scale=zeros,
+            start=True,
+            stop=True,
+        )
         for z in range(PASSES):
             for (c0, n), acc in zip(groups, sums):
                 nc.tensor.matmul_mx(
                     acc[:],
                     lhsT=hid_codes[z][:].bitcast(FP8X4),
-                    lhsT_scale=hid_planes[z][:],
+                    lhsT_scale=hid_planes[z][:, :Q],
                     rhs=words_of(z, c0, n),
                     rhs_scale=voc_planes[z][:, c0 : c0 + n],
                     start=(z == 0),

@@ -34,11 +34,7 @@ def tile_attend_beamvocab_kernel(tc, hid, voc_words, voc_scales, bonus, offs, ou
         keep = ctx.enter_context(tc.tile_pool(name="keep", bufs=1))
         psum = ctx.enter_context(tc.psum_pool(name="psum", bufs=1))
 
-        voc_planes = []
-        for z in range(PASSES):
-            voc_plane = keep.tile([P, V], U8, name="voc_plane%d" % z, align_bytes=64)
-            nc.vector.memset(voc_plane[:].bitcast(I32), 0)
-            voc_planes.append(voc_plane)
+        voc_planes = [keep.tile([P, V], U8, name="voc_plane%d" % z, align_bytes=64) for z in range(PASSES)]
 
         hid_rows = {}
         word_tiles = {}
@@ -82,9 +78,12 @@ def tile_attend_beamvocab_kernel(tc, hid, voc_words, voc_scales, bonus, offs, ou
         zeros = hid_planes[0][:, Q:]
         nc.vector.memset(zeros.bitcast(I32), 0)
 
+        spread = keep.tile([P, V], F32, name="spread")
+        nc.vector.memset(spread[:], 0.0)
+
         hid_codes = []
         for z in range(PASSES):
-            grouped = keep.tile([P, Q, PACK], BF16, name="grouped%d" % z, tag="grouped%d" % z, align_bytes=64)
+            grouped = keep.tile([P, Q, PACK], BF16, name="grouped%d" % z, align_bytes=64)
             nc.vector.tensor_copy(
                 grouped[:].rearrange("p (c i) t -> p c t i", i=4),
                 hid_rows[z][:].rearrange("p t (c i) -> p c t i", i=4),
@@ -92,9 +91,6 @@ def tile_attend_beamvocab_kernel(tc, hid, voc_words, voc_scales, bonus, offs, ou
             codes = keep.tile([P, Q], U32, name="hid_codes%d" % z, align_bytes=64)
             nc.vector.quantize_mx(codes[:].bitcast(FP8X4), hid_planes[z][:, :Q], grouped[:].rearrange("p q t -> p (q t)"))
             hid_codes.append(codes)
-
-        spread = keep.tile([P, V], F32, name="spread", tag="grouped0", align_bytes=64)
-        nc.vector.memset(spread[:], 0.0)
 
         groups = [(c0, BANK) for c0 in range(0, V - BANK, BANK)]
         groups = groups + [(c0, NARROW) for c0 in range(V - BANK, V, NARROW)]

@@ -25,7 +25,7 @@ WORD_BYTES = 2
 SCALE_ROWS = 4
 BANK = 512
 NARROW = 128
-WORD_PIECES = (((0, 512), (512, 1024), (1024, 2048)), ((0, 1024), (1024, 1536), (1536, 2048)))
+WORD_PIECES = (((0, 512), (512, 2048)), ((0, 1024), (1024, 1536), (1536, 2048)))
 
 
 def tile_attend_beamvocab_kernel(tc, hid, voc_words, voc_scales, bonus, offs, out):
@@ -63,25 +63,21 @@ def tile_attend_beamvocab_kernel(tc, hid, voc_words, voc_scales, bonus, offs, ou
         load_hid(0)
         load_words(0, 0)
         load_scales(0)
+        offsets = keep.tile([P, I // 16], U16, name="offsets")
+        nc.sync.dma_start(offsets[:], offs)
         load_words(0, 1)
         load_hid(1)
-        load_words(0, 2)
         load_scales(1)
         for piece in range(len(WORD_PIECES[1])):
             load_words(1, piece)
-        offsets = keep.tile([P, I // 16], U16, name="offsets")
-        nc.sync.dma_start(offsets[:], offs)
         bonus_sb = keep.tile([P, I], F32, name="bonus_sb")
         nc.sync.dma_start(bonus_sb[:], bonus)
-
-        hid_planes = [keep.tile([P, Q + BANK * (1 - z)], U8, name="hid_plane%d" % z, align_bytes=64) for z in range(PASSES)]
-        zeros = hid_planes[0][:, Q:]
-        nc.vector.memset(zeros.bitcast(I32), 0)
 
         spread = keep.tile([P, V], F32, name="spread")
         nc.vector.memset(spread[:], 0.0)
 
         hid_codes = []
+        hid_planes = []
         for z in range(PASSES):
             grouped = keep.tile([P, Q, PACK], BF16, name="grouped%d" % z, align_bytes=64)
             nc.vector.tensor_copy(
@@ -89,28 +85,20 @@ def tile_attend_beamvocab_kernel(tc, hid, voc_words, voc_scales, bonus, offs, ou
                 hid_rows[z][:].rearrange("p t (c i) -> p c t i", i=4),
             )
             codes = keep.tile([P, Q], U32, name="hid_codes%d" % z, align_bytes=64)
-            nc.vector.quantize_mx(codes[:].bitcast(FP8X4), hid_planes[z][:, :Q], grouped[:].rearrange("p q t -> p (q t)"))
+            plane = keep.tile([P, Q], U8, name="hid_plane%d" % z, align_bytes=64)
+            nc.vector.quantize_mx(codes[:].bitcast(FP8X4), plane[:], grouped[:].rearrange("p q t -> p (q t)"))
             hid_codes.append(codes)
+            hid_planes.append(plane)
 
         groups = [(c0, BANK) for c0 in range(0, V - BANK, BANK)]
         groups = groups + [(c0, NARROW) for c0 in range(V - BANK, V, NARROW)]
         sums = [psum.tile([P, n], F32, name="sums%d" % c0) for c0, n in groups]
-
-        nc.tensor.matmul_mx(
-            sums[0][:],
-            lhsT=zeros.bitcast(FP8X4),
-            lhsT_scale=zeros[:, :Q],
-            rhs=words_of(0, 0, BANK),
-            rhs_scale=zeros,
-            start=True,
-            stop=True,
-        )
         for z in range(PASSES):
             for (c0, n), acc in zip(groups, sums):
                 nc.tensor.matmul_mx(
                     acc[:],
                     lhsT=hid_codes[z][:].bitcast(FP8X4),
-                    lhsT_scale=hid_planes[z][:, :Q],
+                    lhsT_scale=hid_planes[z][:],
                     rhs=words_of(z, c0, n),
                     rhs_scale=voc_planes[z][:, c0 : c0 + n],
                     start=(z == 0),

@@ -25,7 +25,7 @@ WORD_BYTES = 2
 SCALE_ROWS = 4
 BANK = 512
 NARROW = 128
-WORD_PIECES = (((0, 512), (512, 2048)), ((0, 1024), (1024, 1536), (1536, 2048)))
+WORD_PIECES = (((0, 512), (512, 2048)), ((0, 512), (512, 1024), (1024, 2048)))
 
 
 def tile_attend_beamvocab_kernel(tc, hid, voc_words, voc_scales, bonus, offs, out):
@@ -73,32 +73,43 @@ def tile_attend_beamvocab_kernel(tc, hid, voc_words, voc_scales, bonus, offs, ou
         bonus_sb = keep.tile([P, I], F32, name="bonus_sb")
         nc.sync.dma_start(bonus_sb[:], bonus)
 
-        spread = keep.tile([P, V], F32, name="spread")
-        nc.vector.memset(spread[:], 0.0)
+        hid_planes = [keep.tile([P, Q + BANK * (1 - z)], U8, name="hid_plane%d" % z, align_bytes=64) for z in range(PASSES)]
+        zeros = hid_planes[0][:, Q:]
+        nc.vector.memset(zeros.bitcast(I32), 0)
 
         hid_codes = []
-        hid_planes = []
         for z in range(PASSES):
-            grouped = keep.tile([P, Q, PACK], BF16, name="grouped%d" % z, align_bytes=64)
+            grouped = keep.tile([P, Q, PACK], BF16, name="grouped%d" % z, tag="grouped%d" % z, align_bytes=64)
             nc.vector.tensor_copy(
                 grouped[:].rearrange("p (c i) t -> p c t i", i=4),
                 hid_rows[z][:].rearrange("p t (c i) -> p c t i", i=4),
             )
             codes = keep.tile([P, Q], U32, name="hid_codes%d" % z, align_bytes=64)
-            plane = keep.tile([P, Q], U8, name="hid_plane%d" % z, align_bytes=64)
-            nc.vector.quantize_mx(codes[:].bitcast(FP8X4), plane[:], grouped[:].rearrange("p q t -> p (q t)"))
+            nc.vector.quantize_mx(codes[:].bitcast(FP8X4), hid_planes[z][:, :Q], grouped[:].rearrange("p q t -> p (q t)"))
             hid_codes.append(codes)
-            hid_planes.append(plane)
+
+        spread = keep.tile([P, V], F32, name="spread", tag="grouped0", align_bytes=64)
+        nc.vector.memset(spread[:], 0.0)
 
         groups = [(c0, BANK) for c0 in range(0, V - BANK, BANK)]
         groups = groups + [(c0, NARROW) for c0 in range(V - BANK, V, NARROW)]
         sums = [psum.tile([P, n], F32, name="sums%d" % c0) for c0, n in groups]
+
+        nc.tensor.matmul_mx(
+            sums[0][:],
+            lhsT=zeros.bitcast(FP8X4),
+            lhsT_scale=zeros[:, :Q],
+            rhs=words_of(0, 0, BANK),
+            rhs_scale=zeros,
+            start=True,
+            stop=True,
+        )
         for z in range(PASSES):
             for (c0, n), acc in zip(groups, sums):
                 nc.tensor.matmul_mx(
                     acc[:],
                     lhsT=hid_codes[z][:].bitcast(FP8X4),
-                    lhsT_scale=hid_planes[z][:],
+                    lhsT_scale=hid_planes[z][:, :Q],
                     rhs=words_of(z, c0, n),
                     rhs_scale=voc_planes[z][:, c0 : c0 + n],
                     start=(z == 0),

@@ -25,7 +25,7 @@ WORD_BYTES = 2
 SCALE_ROWS = 4
 BANK = 512
 NARROW = 128
-WORD_PIECES = (((0, 512), (512, 2048)), ((0, 512), (512, 1024), (1024, 2048)))
+SCALE_RANGES = ((0, 1024), (1024, 2048))
 
 
 def tile_attend_beamvocab_kernel(tc, hid, voc_words, voc_scales, bonus, offs, out):
@@ -34,52 +34,65 @@ def tile_attend_beamvocab_kernel(tc, hid, voc_words, voc_scales, bonus, offs, ou
         keep = ctx.enter_context(tc.tile_pool(name="keep", bufs=1))
         psum = ctx.enter_context(tc.psum_pool(name="psum", bufs=1))
 
-        voc_planes = [keep.tile([P, V], U8, name="voc_plane%d" % z, align_bytes=64) for z in range(PASSES)]
-
         hid_rows = {}
         word_tiles = {}
+        voc_planes = {}
 
         def load_hid(z):
             hid_rows[z] = keep.tile([P, PACK, Q], F32, name="hid_rows%d" % z)
             rows = hid[z * K_PASS : (z + 1) * K_PASS, :]
             nc.sync.dma_start(hid_rows[z][:], rows.rearrange("(p t) q -> p t q", t=PACK))
 
-        def load_words(z, piece):
-            lo, hi = WORD_PIECES[z][piece]
-            tile = keep.tile([P, WORD_BYTES * (hi - lo)], U8, name="words%d_%d" % (z, piece), align_bytes=64)
-            nc.sync.dma_start(tile[:].bitcast(I32), voc_words[z, :, WORD_BYTES * lo : WORD_BYTES * hi].bitcast(I32))
-            word_tiles[z, piece] = tile
+        def load_words(passes, c0):
+            z0, count = passes[0], len(passes)
+            tile = keep.tile([P, count, WORD_BYTES * BANK], U8, name="words%d_%d" % (z0, c0), align_bytes=64)
+            rows = voc_words[z0 : z0 + count, :, WORD_BYTES * c0 : WORD_BYTES * (c0 + BANK)].bitcast(I32)
+            nc.sync.dma_start(tile[:].bitcast(I32), rows.rearrange("z p c -> p z c"))
+            for j, z in enumerate(passes):
+                word_tiles[z, c0] = tile[:, j, :]
 
         def words_of(z, c0, n):
-            piece = max(k for k, (lo, hi) in enumerate(WORD_PIECES[z]) if lo <= c0)
-            at = c0 - WORD_PIECES[z][piece][0]
-            return word_tiles[z, piece][:, WORD_BYTES * at : WORD_BYTES * (at + n)].bitcast(FP4X4)
+            at = c0 % BANK
+            return word_tiles[z, c0 - at][:, WORD_BYTES * at : WORD_BYTES * (at + n)].bitcast(FP4X4)
 
-        def load_scales(z):
-            scale_rows = voc_scales[z].bitcast(I32).rearrange("(a r) c -> r a c", r=SCALE_ROWS)
+        def load_scales(k):
+            lo, hi = SCALE_RANGES[k]
+            plane = keep.tile([P, PASSES, hi - lo], U8, name="voc_plane%d" % k, align_bytes=64)
+            rows = voc_scales[:, :, lo:hi].bitcast(I32).rearrange("z (a r) c -> r a z c", r=SCALE_ROWS)
             for r in range(SCALE_ROWS):
-                nc.sync.dma_start(voc_planes[z][:].bitcast(I32)[r:P:32, :], scale_rows[r])
+                nc.sync.dma_start(plane[:].bitcast(I32)[r:P:32, :, :], rows[r])
+            voc_planes[k] = plane
+
+        def scales_of(z, c0, n):
+            k = max(k for k, (lo, hi) in enumerate(SCALE_RANGES) if lo <= c0)
+            at = c0 - SCALE_RANGES[k][0]
+            return voc_planes[k][:, z, at : at + n]
 
         load_hid(0)
-        load_words(0, 0)
-        load_scales(0)
-        offsets = keep.tile([P, I // 16], U16, name="offsets")
-        nc.sync.dma_start(offsets[:], offs)
-        load_words(0, 1)
         load_hid(1)
+        load_scales(0)
+        load_words((0, 1), 0)
+        load_words((0, 1), BANK)
         load_scales(1)
-        for piece in range(len(WORD_PIECES[1])):
-            load_words(1, piece)
+        for c0 in (2 * BANK, 3 * BANK):
+            for z in range(PASSES):
+                load_words((z,), c0)
         bonus_sb = keep.tile([P, I], F32, name="bonus_sb")
         nc.sync.dma_start(bonus_sb[:], bonus)
+        offsets = keep.tile([P, I // 16], U16, name="offsets")
+        nc.sync.dma_start(offsets[:], offs)
 
-        hid_planes = [keep.tile([P, Q + BANK * (1 - z)], U8, name="hid_plane%d" % z, align_bytes=64) for z in range(PASSES)]
+        spread = keep.tile([P, V], F32, name="spread", align_bytes=64)
+        nc.vector.memset(spread[:], 0.0)
+
+        spare = WORD_BYTES * BANK
+        hid_planes = [keep.tile([P, Q + spare * (1 - z)], U8, name="hid_plane%d" % z, align_bytes=64) for z in range(PASSES)]
         zeros = hid_planes[0][:, Q:]
         nc.vector.memset(zeros.bitcast(I32), 0)
 
         hid_codes = []
         for z in range(PASSES):
-            grouped = keep.tile([P, Q, PACK], BF16, name="grouped%d" % z, tag="grouped%d" % z, align_bytes=64)
+            grouped = keep.tile([P, Q, PACK], BF16, name="grouped%d" % z, align_bytes=64)
             nc.vector.tensor_copy(
                 grouped[:].rearrange("p (c i) t -> p c t i", i=4),
                 hid_rows[z][:].rearrange("p t (c i) -> p c t i", i=4),
@@ -88,41 +101,42 @@ def tile_attend_beamvocab_kernel(tc, hid, voc_words, voc_scales, bonus, offs, ou
             nc.vector.quantize_mx(codes[:].bitcast(FP8X4), hid_planes[z][:, :Q], grouped[:].rearrange("p q t -> p (q t)"))
             hid_codes.append(codes)
 
-        spread = keep.tile([P, V], F32, name="spread", tag="grouped0", align_bytes=64)
-        nc.vector.memset(spread[:], 0.0)
-
-        groups = [(c0, BANK) for c0 in range(0, V - BANK, BANK)]
-        groups = groups + [(c0, NARROW) for c0 in range(V - BANK, V, NARROW)]
-        sums = [psum.tile([P, n], F32, name="sums%d" % c0) for c0, n in groups]
-
-        nc.tensor.matmul_mx(
-            sums[0][:],
-            lhsT=zeros.bitcast(FP8X4),
-            lhsT_scale=zeros[:, :Q],
-            rhs=words_of(0, 0, BANK),
-            rhs_scale=zeros,
-            start=True,
-            stop=True,
-        )
-        for z in range(PASSES):
-            for (c0, n), acc in zip(groups, sums):
-                nc.tensor.matmul_mx(
-                    acc[:],
-                    lhsT=hid_codes[z][:].bitcast(FP8X4),
-                    lhsT_scale=hid_planes[z][:, :Q],
-                    rhs=words_of(z, c0, n),
-                    rhs_scale=voc_planes[z][:, c0 : c0 + n],
-                    start=(z == 0),
-                    stop=(z == PASSES - 1),
-                )
-
-        on_scalar = (0, 2, len(groups) - 1)
         logits = keep.tile([P, V], F32, name="logits")
-        for g, ((c0, n), acc) in enumerate(zip(groups, sums)):
-            if g in on_scalar:
-                nc.scalar.activation(logits[:, c0 : c0 + n], acc[:], ACT.Copy)
-            else:
-                nc.vector.tensor_copy(logits[:, c0 : c0 + n], acc[:])
+        stretches = [[(c0, BANK)] for c0 in (0, BANK)]
+        stretches = stretches + [[(c, NARROW) for c in range(c0, c0 + BANK, NARROW)] for c0 in (2 * BANK, 3 * BANK)]
+        g = 0
+        for stretch in stretches:
+            sums = []
+            for j, (c0, n) in enumerate(stretch):
+                sums.append(psum.tile([P, BANK], F32, name="sums%d" % c0, tag="bank%d" % ((g + j) % 8)))
+            if g == 0:
+                for w in range(2):
+                    nc.tensor.matmul_mx(
+                        sums[0][:],
+                        lhsT=zeros[:, : 4 * Q].bitcast(FP8X4),
+                        lhsT_scale=zeros[:, :Q],
+                        rhs=zeros.bitcast(FP4X4),
+                        rhs_scale=zeros[:, :BANK],
+                        start=True,
+                        stop=True,
+                    )
+            for z in range(PASSES):
+                for (c0, n), acc in zip(stretch, sums):
+                    nc.tensor.matmul_mx(
+                        acc[:, :n],
+                        lhsT=hid_codes[z][:].bitcast(FP8X4),
+                        lhsT_scale=hid_planes[z][:, :Q],
+                        rhs=words_of(z, c0, n),
+                        rhs_scale=scales_of(z, c0, n),
+                        start=(z == 0),
+                        stop=(z == PASSES - 1),
+                    )
+            for j, ((c0, n), acc) in enumerate(zip(stretch, sums)):
+                if (g + j) % 2 == 0:
+                    nc.scalar.activation(logits[:, c0 : c0 + n], acc[:, :n], ACT.Copy)
+                else:
+                    nc.vector.tensor_copy(logits[:, c0 : c0 + n], acc[:, :n])
+            g = g + len(stretch)
 
         scores = keep.tile([P, I], F32, name="scores")
         nc.vector.tensor_tensor(scores[:], logits[:].indirect(offsets[:]), bonus_sb[:], ALU.add)

@@ -25,7 +25,7 @@ WORD_BYTES = 2
 SCALE_ROWS = 4
 BANK = 512
 NARROW = 128
-SCALE_RANGES = ((0, 1024), (1024, 2048))
+STRETCHES = (512, 512, 384, 384, 256)
 
 
 def tile_attend_beamvocab_kernel(tc, hid, voc_words, voc_scales, bonus, offs, out):
@@ -36,47 +36,27 @@ def tile_attend_beamvocab_kernel(tc, hid, voc_words, voc_scales, bonus, offs, ou
 
         hid_rows = {}
         word_tiles = {}
-        voc_planes = {}
 
         def load_hid(z):
-            hid_rows[z] = keep.tile([P, PACK, Q], F32, name="hid_rows%d" % z)
+            hid_rows[z] = keep.tile([P, PACK, Q], F32, name="hid_rows%d" % z, tag="hid_rows%d" % z, align_bytes=64)
             rows = hid[z * K_PASS : (z + 1) * K_PASS, :]
             nc.sync.dma_start(hid_rows[z][:], rows.rearrange("(p t) q -> p t q", t=PACK))
 
-        def load_words(passes, c0):
-            z0, count = passes[0], len(passes)
-            tile = keep.tile([P, count, WORD_BYTES * BANK], U8, name="words%d_%d" % (z0, c0), align_bytes=64)
-            rows = voc_words[z0 : z0 + count, :, WORD_BYTES * c0 : WORD_BYTES * (c0 + BANK)].bitcast(I32)
+        def load_words(c0, n):
+            tile = keep.tile([P, PASSES, WORD_BYTES * n], U8, name="words%d" % c0, align_bytes=64)
+            rows = voc_words[:, :, WORD_BYTES * c0 : WORD_BYTES * (c0 + n)].bitcast(I32)
             nc.sync.dma_start(tile[:].bitcast(I32), rows.rearrange("z p c -> p z c"))
-            for j, z in enumerate(passes):
-                word_tiles[z, c0] = tile[:, j, :]
-
-        def words_of(z, c0, n):
-            at = c0 % BANK
-            return word_tiles[z, c0 - at][:, WORD_BYTES * at : WORD_BYTES * (at + n)].bitcast(FP4X4)
-
-        def load_scales(k):
-            lo, hi = SCALE_RANGES[k]
-            plane = keep.tile([P, PASSES, hi - lo], U8, name="voc_plane%d" % k, align_bytes=64)
-            rows = voc_scales[:, :, lo:hi].bitcast(I32).rearrange("z (a r) c -> r a z c", r=SCALE_ROWS)
-            for r in range(SCALE_ROWS):
-                nc.sync.dma_start(plane[:].bitcast(I32)[r:P:32, :, :], rows[r])
-            voc_planes[k] = plane
-
-        def scales_of(z, c0, n):
-            k = max(k for k, (lo, hi) in enumerate(SCALE_RANGES) if lo <= c0)
-            at = c0 - SCALE_RANGES[k][0]
-            return voc_planes[k][:, z, at : at + n]
+            word_tiles[c0] = tile
 
         load_hid(0)
         load_hid(1)
-        load_scales(0)
-        load_words((0, 1), 0)
-        load_words((0, 1), BANK)
-        load_scales(1)
-        for c0 in (2 * BANK, 3 * BANK):
-            for z in range(PASSES):
-                load_words((z,), c0)
+        voc_plane = keep.tile([P, PASSES, V], U8, name="voc_plane", align_bytes=64)
+        scale_rows = voc_scales.bitcast(I32).rearrange("z (a r) c -> r a z c", r=SCALE_ROWS)
+        for r in range(SCALE_ROWS):
+            nc.sync.dma_start(voc_plane[:].bitcast(I32)[r:P:32, :, :], scale_rows[r])
+        starts = [sum(STRETCHES[:k]) for k in range(len(STRETCHES))]
+        for c0, n in zip(starts, STRETCHES):
+            load_words(c0, n)
         bonus_sb = keep.tile([P, I], F32, name="bonus_sb")
         nc.sync.dma_start(bonus_sb[:], bonus)
         offsets = keep.tile([P, I // 16], U16, name="offsets")
@@ -86,26 +66,28 @@ def tile_attend_beamvocab_kernel(tc, hid, voc_words, voc_scales, bonus, offs, ou
         nc.vector.memset(spread[:], 0.0)
 
         spare = WORD_BYTES * BANK
-        hid_planes = [keep.tile([P, Q + spare * (1 - z)], U8, name="hid_plane%d" % z, align_bytes=64) for z in range(PASSES)]
-        zeros = hid_planes[0][:, Q:]
-        nc.vector.memset(zeros.bitcast(I32), 0)
-
         hid_codes = []
+        hid_planes = []
         for z in range(PASSES):
             grouped = keep.tile([P, Q, PACK], BF16, name="grouped%d" % z, align_bytes=64)
             nc.vector.tensor_copy(
                 grouped[:].rearrange("p (c i) t -> p c t i", i=4),
                 hid_rows[z][:].rearrange("p t (c i) -> p c t i", i=4),
             )
+            plane = keep.tile([P, Q + spare * (1 - z)], U8, name="hid_plane%d" % z, tag="hid_rows%d" % z, align_bytes=64)
+            if z == 0:
+                zeros = plane[:, Q:]
+                nc.vector.memset(zeros.bitcast(I32), 0)
             codes = keep.tile([P, Q], U32, name="hid_codes%d" % z, align_bytes=64)
-            nc.vector.quantize_mx(codes[:].bitcast(FP8X4), hid_planes[z][:, :Q], grouped[:].rearrange("p q t -> p (q t)"))
+            nc.vector.quantize_mx(codes[:].bitcast(FP8X4), plane[:, :Q], grouped[:].rearrange("p q t -> p (q t)"))
             hid_codes.append(codes)
+            hid_planes.append(plane)
 
         logits = keep.tile([P, V], F32, name="logits")
-        stretches = [[(c0, BANK)] for c0 in (0, BANK)]
-        stretches = stretches + [[(c, NARROW) for c in range(c0, c0 + BANK, NARROW)] for c0 in (2 * BANK, 3 * BANK)]
         g = 0
-        for stretch in stretches:
+        for first, width in zip(starts, STRETCHES):
+            step = BANK if width == BANK else NARROW
+            stretch = [(c0, step) for c0 in range(first, first + width, step)]
             sums = []
             for j, (c0, n) in enumerate(stretch):
                 sums.append(psum.tile([P, BANK], F32, name="sums%d" % c0, tag="bank%d" % ((g + j) % 8)))
@@ -126,8 +108,8 @@ def tile_attend_beamvocab_kernel(tc, hid, voc_words, voc_scales, bonus, offs, ou
                         acc[:, :n],
                         lhsT=hid_codes[z][:].bitcast(FP8X4),
                         lhsT_scale=hid_planes[z][:, :Q],
-                        rhs=words_of(z, c0, n),
-                        rhs_scale=scales_of(z, c0, n),
+                        rhs=word_tiles[first][:, z, WORD_BYTES * (c0 - first) : WORD_BYTES * (c0 - first + n)].bitcast(FP4X4),
+                        rhs_scale=voc_plane[:, z, c0 : c0 + n],
                         start=(z == 0),
                         stop=(z == PASSES - 1),
                     )

@@ -38,7 +38,7 @@ def tile_attend_beamvocab_kernel(tc, hid, voc_words, voc_scales, bonus, offs, ou
         word_tiles = {}
 
         def load_hid(z):
-            hid_rows[z] = keep.tile([P, PACK, Q], F32, name="hid_rows%d" % z, tag="hid_rows%d" % z, align_bytes=64)
+            hid_rows[z] = keep.tile([P, PACK, Q], F32, name="hid_rows%d" % z)
             rows = hid[z * K_PASS : (z + 1) * K_PASS, :]
             nc.sync.dma_start(hid_rows[z][:], rows.rearrange("(p t) q -> p t q", t=PACK))
 
@@ -48,12 +48,12 @@ def tile_attend_beamvocab_kernel(tc, hid, voc_words, voc_scales, bonus, offs, ou
             nc.sync.dma_start(tile[:].bitcast(I32), rows.rearrange("z p c -> p z c"))
             word_tiles[c0] = tile
 
-        load_hid(0)
-        load_hid(1)
         voc_plane = keep.tile([P, PASSES, V], U8, name="voc_plane", align_bytes=64)
         scale_rows = voc_scales.bitcast(I32).rearrange("z (a r) c -> r a z c", r=SCALE_ROWS)
         for r in range(SCALE_ROWS):
             nc.sync.dma_start(voc_plane[:].bitcast(I32)[r:P:32, :, :], scale_rows[r])
+        load_hid(0)
+        load_hid(1)
         starts = [sum(STRETCHES[:k]) for k in range(len(STRETCHES))]
         for c0, n in zip(starts, STRETCHES):
             load_words(c0, n)
@@ -66,22 +66,20 @@ def tile_attend_beamvocab_kernel(tc, hid, voc_words, voc_scales, bonus, offs, ou
         nc.vector.memset(spread[:], 0.0)
 
         spare = WORD_BYTES * BANK
+        hid_planes = [keep.tile([P, Q + spare * (1 - z)], U8, name="hid_plane%d" % z, align_bytes=64) for z in range(PASSES)]
+        zeros = hid_planes[0][:, Q:]
+        nc.vector.memset(zeros.bitcast(I32), 0)
+
         hid_codes = []
-        hid_planes = []
         for z in range(PASSES):
             grouped = keep.tile([P, Q, PACK], BF16, name="grouped%d" % z, align_bytes=64)
             nc.vector.tensor_copy(
                 grouped[:].rearrange("p (c i) t -> p c t i", i=4),
                 hid_rows[z][:].rearrange("p t (c i) -> p c t i", i=4),
             )
-            plane = keep.tile([P, Q + spare * (1 - z)], U8, name="hid_plane%d" % z, tag="hid_rows%d" % z, align_bytes=64)
-            if z == 0:
-                zeros = plane[:, Q:]
-                nc.vector.memset(zeros.bitcast(I32), 0)
             codes = keep.tile([P, Q], U32, name="hid_codes%d" % z, align_bytes=64)
-            nc.vector.quantize_mx(codes[:].bitcast(FP8X4), plane[:, :Q], grouped[:].rearrange("p q t -> p (q t)"))
+            nc.vector.quantize_mx(codes[:].bitcast(FP8X4), hid_planes[z][:, :Q], grouped[:].rearrange("p q t -> p (q t)"))
             hid_codes.append(codes)
-            hid_planes.append(plane)
 
         logits = keep.tile([P, V], F32, name="logits")
         g = 0
@@ -98,7 +96,7 @@ def tile_attend_beamvocab_kernel(tc, hid, voc_words, voc_scales, bonus, offs, ou
                         lhsT=zeros[:, : 4 * Q].bitcast(FP8X4),
                         lhsT_scale=zeros[:, :Q],
                         rhs=zeros.bitcast(FP4X4),
-                        rhs_scale=zeros[:, :BANK],
+                        rhs_scale=voc_plane[:, 0, :BANK],
                         start=True,
                         stop=True,
                     )

@@ -25,7 +25,8 @@ WORD_BYTES = 2
 SCALE_ROWS = 4
 BANK = 512
 NARROW = 128
-STRETCHES = (512, 512, 384, 384, 256)
+STRETCHES = (384, 512, 512, 384, 256)
+CAST_SPLIT = 88
 
 
 def tile_attend_beamvocab_kernel(tc, hid, voc_words, voc_scales, bonus, offs, out):
@@ -74,8 +75,12 @@ def tile_attend_beamvocab_kernel(tc, hid, voc_words, voc_scales, bonus, offs, ou
         for z in range(PASSES):
             grouped = keep.tile([P, Q, PACK], BF16, name="grouped%d" % z, align_bytes=64)
             nc.vector.tensor_copy(
-                grouped[:].rearrange("p (c i) t -> p c t i", i=4),
-                hid_rows[z][:].rearrange("p t (c i) -> p c t i", i=4),
+                grouped[:, :CAST_SPLIT, :].rearrange("p (c i) t -> p c t i", i=4),
+                hid_rows[z][:, :, :CAST_SPLIT].rearrange("p t (c i) -> p c t i", i=4),
+            )
+            nc.scalar.copy(
+                grouped[:, CAST_SPLIT:, :].rearrange("p (c i) t -> p c t i", i=4),
+                hid_rows[z][:, :, CAST_SPLIT:].rearrange("p t (c i) -> p c t i", i=4),
             )
             codes = keep.tile([P, Q], U32, name="hid_codes%d" % z, align_bytes=64)
             nc.vector.quantize_mx(codes[:].bitcast(FP8X4), hid_planes[z][:, :Q], grouped[:].rearrange("p q t -> p (q t)"))

@@ -22,11 +22,16 @@ PACK = 4
 K_PASS = P * PACK
 PASSES = D // K_PASS
 WORD_BYTES = 2
+LINE = 4
+GROUP_ROWS = 16
+QUADRANT = 32
 SCALE_ROWS = 4
 BANK = 512
+BANKS = 8
 NARROW = 128
+WARM_UPS = 2
 STRETCHES = (384, 512, 512, 384, 256)
-CAST_SPLIT = 88
+CAST_SPLIT = 80
 
 
 def tile_attend_beamvocab_kernel(tc, hid, voc_words, voc_scales, bonus, offs, out):
@@ -35,93 +40,89 @@ def tile_attend_beamvocab_kernel(tc, hid, voc_words, voc_scales, bonus, offs, ou
         keep = ctx.enter_context(tc.tile_pool(name="keep", bufs=1))
         psum = ctx.enter_context(tc.psum_pool(name="psum", bufs=1))
 
-        hid_rows = {}
-        word_tiles = {}
-
-        def load_hid(z):
-            hid_rows[z] = keep.tile([P, PACK, Q], F32, name="hid_rows%d" % z)
-            rows = hid[z * K_PASS : (z + 1) * K_PASS, :]
-            nc.sync.dma_start(hid_rows[z][:], rows.rearrange("(p t) q -> p t q", t=PACK))
-
-        def load_words(c0, n):
-            tile = keep.tile([P, PASSES, WORD_BYTES * n], U8, name="words%d" % c0, align_bytes=64)
-            rows = voc_words[:, :, WORD_BYTES * c0 : WORD_BYTES * (c0 + n)].bitcast(I32)
-            nc.sync.dma_start(tile[:].bitcast(I32), rows.rearrange("z p c -> p z c"))
-            word_tiles[c0] = tile
-
-        voc_plane = keep.tile([P, PASSES, V], U8, name="voc_plane", align_bytes=64)
+        voc_scale_sb = keep.tile([P, PASSES, V], U8, name="voc_plane", align_bytes=64)
         scale_rows = voc_scales.bitcast(I32).rearrange("z (a r) c -> r a z c", r=SCALE_ROWS)
         for r in range(SCALE_ROWS):
-            nc.sync.dma_start(voc_plane[:].bitcast(I32)[r:P:32, :, :], scale_rows[r])
-        load_hid(0)
-        load_hid(1)
+            nc.sync.dma_start(voc_scale_sb[:].bitcast(I32)[r:P:QUADRANT, :, :], scale_rows[r])
+
+        hid_rows = []
+        for z in range(PASSES):
+            rows_sb = keep.tile([P, PACK, Q], F32, name="hid_rows%d" % z)
+            nc.sync.dma_start(rows_sb[:], hid[z * K_PASS : (z + 1) * K_PASS, :].rearrange("(p t) q -> p t q", t=PACK))
+            hid_rows.append(rows_sb)
+
         starts = [sum(STRETCHES[:k]) for k in range(len(STRETCHES))]
-        for c0, n in zip(starts, STRETCHES):
-            load_words(c0, n)
+        stretch_words = []
+        for first, width in zip(starts, STRETCHES):
+            words_sb = keep.tile([P, PASSES, WORD_BYTES * width], U8, name="words%d" % first, align_bytes=64)
+            words_hbm = voc_words[:, :, WORD_BYTES * first : WORD_BYTES * (first + width)].bitcast(I32)
+            nc.sync.dma_start(words_sb[:].bitcast(I32), words_hbm.rearrange("z p c -> p z c"))
+            stretch_words.append(words_sb)
+
         bonus_sb = keep.tile([P, I], F32, name="bonus_sb")
         nc.sync.dma_start(bonus_sb[:], bonus)
-        offsets = keep.tile([P, I // 16], U16, name="offsets")
+        offsets = keep.tile([P, I // GROUP_ROWS], U16, name="offsets")
         nc.sync.dma_start(offsets[:], offs)
 
         spread = keep.tile([P, V], F32, name="spread", align_bytes=64)
         nc.vector.memset(spread[:], 0.0)
 
-        spare = WORD_BYTES * BANK
-        hid_planes = [keep.tile([P, Q + spare * (1 - z)], U8, name="hid_plane%d" % z, align_bytes=64) for z in range(PASSES)]
-        zeros = hid_planes[0][:, Q:]
+        spare = (WORD_BYTES * BANK, 0)
+        hid_scale_sb = [keep.tile([P, Q + spare[z]], U8, name="hid_plane%d" % z, align_bytes=64) for z in range(PASSES)]
+        zeros = hid_scale_sb[0][:, Q:]
         nc.vector.memset(zeros.bitcast(I32), 0)
 
         hid_codes = []
         for z in range(PASSES):
             grouped = keep.tile([P, Q, PACK], BF16, name="grouped%d" % z, align_bytes=64)
             nc.vector.tensor_copy(
-                grouped[:, :CAST_SPLIT, :].rearrange("p (c i) t -> p c t i", i=4),
-                hid_rows[z][:, :, :CAST_SPLIT].rearrange("p t (c i) -> p c t i", i=4),
+                grouped[:, :CAST_SPLIT, :].rearrange("p (c i) t -> p c t i", i=LINE),
+                hid_rows[z][:, :, :CAST_SPLIT].rearrange("p t (c i) -> p c t i", i=LINE),
             )
             nc.scalar.copy(
-                grouped[:, CAST_SPLIT:, :].rearrange("p (c i) t -> p c t i", i=4),
-                hid_rows[z][:, :, CAST_SPLIT:].rearrange("p t (c i) -> p c t i", i=4),
+                grouped[:, CAST_SPLIT:, :].rearrange("p (c i) t -> p c t i", i=LINE),
+                hid_rows[z][:, :, CAST_SPLIT:].rearrange("p t (c i) -> p c t i", i=LINE),
             )
             codes = keep.tile([P, Q], U32, name="hid_codes%d" % z, align_bytes=64)
-            nc.vector.quantize_mx(codes[:].bitcast(FP8X4), hid_planes[z][:, :Q], grouped[:].rearrange("p q t -> p (q t)"))
+            nc.vector.quantize_mx(codes[:].bitcast(FP8X4), hid_scale_sb[z][:, :Q], grouped[:].rearrange("p q t -> p (q t)"))
             hid_codes.append(codes)
 
         logits = keep.tile([P, V], F32, name="logits")
-        g = 0
-        for first, width in zip(starts, STRETCHES):
-            step = BANK if width == BANK else NARROW
-            stretch = [(c0, step) for c0 in range(first, first + width, step)]
-            sums = []
-            for j, (c0, n) in enumerate(stretch):
-                sums.append(psum.tile([P, BANK], F32, name="sums%d" % c0, tag="bank%d" % ((g + j) % 8)))
-            if g == 0:
-                for w in range(2):
+        groups_before = 0
+        for first, width, words_sb in zip(starts, STRETCHES, stretch_words):
+            n = BANK if width == BANK else NARROW
+            columns = list(range(first, first + width, n))
+            numbers = range(groups_before, groups_before + len(columns))
+            sums = [psum.tile([P, BANK], F32, name="sums%d" % c0, tag="bank%d" % (g % BANKS)) for g, c0 in zip(numbers, columns)]
+            if first == 0:
+                for warm_up in range(WARM_UPS):
                     nc.tensor.matmul_mx(
                         sums[0][:],
-                        lhsT=zeros[:, : 4 * Q].bitcast(FP8X4),
+                        lhsT=zeros[:, : PACK * Q].bitcast(FP8X4),
                         lhsT_scale=zeros[:, :Q],
                         rhs=zeros.bitcast(FP4X4),
-                        rhs_scale=voc_plane[:, 0, :BANK],
+                        rhs_scale=voc_scale_sb[:, 0, :BANK],
                         start=True,
                         stop=True,
                     )
             for z in range(PASSES):
-                for (c0, n), acc in zip(stretch, sums):
+                for c0, acc in zip(columns, sums):
+                    at = WORD_BYTES * (c0 - first)
                     nc.tensor.matmul_mx(
                         acc[:, :n],
                         lhsT=hid_codes[z][:].bitcast(FP8X4),
-                        lhsT_scale=hid_planes[z][:, :Q],
-                        rhs=word_tiles[first][:, z, WORD_BYTES * (c0 - first) : WORD_BYTES * (c0 - first + n)].bitcast(FP4X4),
-                        rhs_scale=voc_plane[:, z, c0 : c0 + n],
+                        lhsT_scale=hid_scale_sb[z][:, :Q],
+                        rhs=words_sb[:, z, at : at + WORD_BYTES * n].bitcast(FP4X4),
+                        rhs_scale=voc_scale_sb[:, z, c0 : c0 + n],
                         start=(z == 0),
                         stop=(z == PASSES - 1),
                     )
-            for j, ((c0, n), acc) in enumerate(zip(stretch, sums)):
-                if (g + j) % 2 == 0:
+            for g, c0, acc in zip(numbers, columns, sums):
+                if g % 2 == 1:
                     nc.scalar.activation(logits[:, c0 : c0 + n], acc[:, :n], ACT.Copy)
                 else:
                     nc.vector.tensor_copy(logits[:, c0 : c0 + n], acc[:, :n])
-            g = g + len(stretch)
+            groups_before = groups_before + len(columns)
 
         scores = keep.tile([P, I], F32, name="scores")
         nc.vector.tensor_tensor(scores[:], logits[:].indirect(offsets[:]), bonus_sb[:], ALU.add)

@@ -30,7 +30,7 @@ BANK = 512
 BANKS = 8
 NARROW = 128
 WARM_UPS = 2
-STRETCHES = (384, 512, 512, 384, 256)
+STRETCHES = (256, 512, 512, 384, 384)
 CAST_SPLIT = 80
 
 
@@ -40,37 +40,41 @@ def tile_attend_beamvocab_kernel(tc, hid, voc_words, voc_scales, bonus, offs, ou
         keep = ctx.enter_context(tc.tile_pool(name="keep", bufs=1))
         psum = ctx.enter_context(tc.psum_pool(name="psum", bufs=1))
 
-        voc_scale_sb = keep.tile([P, PASSES, V], U8, name="voc_plane", align_bytes=64)
-        scale_rows = voc_scales.bitcast(I32).rearrange("z (a r) c -> r a z c", r=SCALE_ROWS)
-        for r in range(SCALE_ROWS):
-            nc.sync.dma_start(voc_scale_sb[:].bitcast(I32)[r:P:QUADRANT, :, :], scale_rows[r])
-
-        hid_rows = []
-        for z in range(PASSES):
+        def load_hid(z):
             rows_sb = keep.tile([P, PACK, Q], F32, name="hid_rows%d" % z)
             nc.sync.dma_start(rows_sb[:], hid[z * K_PASS : (z + 1) * K_PASS, :].rearrange("(p t) q -> p t q", t=PACK))
-            hid_rows.append(rows_sb)
+            return rows_sb
 
-        starts = [sum(STRETCHES[:k]) for k in range(len(STRETCHES))]
-        stretch_words = []
-        for first, width in zip(starts, STRETCHES):
+        def load_words(first, width):
             words_sb = keep.tile([P, PASSES, WORD_BYTES * width], U8, name="words%d" % first, align_bytes=64)
             words_hbm = voc_words[:, :, WORD_BYTES * first : WORD_BYTES * (first + width)].bitcast(I32)
             nc.sync.dma_start(words_sb[:].bitcast(I32), words_hbm.rearrange("z p c -> p z c"))
-            stretch_words.append(words_sb)
+            return words_sb
 
-        bonus_sb = keep.tile([P, I], F32, name="bonus_sb")
-        nc.sync.dma_start(bonus_sb[:], bonus)
+        starts = [sum(STRETCHES[:k]) for k in range(len(STRETCHES))]
+        hid_rows = [load_hid(0)]
+        stretch_words = [load_words(starts[0], STRETCHES[0])]
+        hid_rows.append(load_hid(1))
+
+        voc_scale_sb = keep.tile([P, PASSES, V], U8, name="voc_plane", align_bytes=64)
+        scale_rows = voc_scales.bitcast(I32).rearrange("z (a r) c -> r a z c", r=SCALE_ROWS)
+        last = SCALE_ROWS - 1
+        for r in range(last):
+            nc.sync.dma_start(voc_scale_sb[:].bitcast(I32)[r:P:QUADRANT, :, :], scale_rows[r])
+        for z in range(PASSES):
+            nc.sync.dma_start(voc_scale_sb[:].bitcast(I32)[last:P:QUADRANT, z, :], scale_rows[last][:, z, :])
         offsets = keep.tile([P, I // GROUP_ROWS], U16, name="offsets")
         nc.sync.dma_start(offsets[:], offs)
+
+        for first, width in zip(starts[1:], STRETCHES[1:]):
+            stretch_words.append(load_words(first, width))
+        bonus_sb = keep.tile([P, I], F32, name="bonus_sb")
+        nc.sync.dma_start(bonus_sb[:], bonus)
 
         spread = keep.tile([P, V], F32, name="spread", align_bytes=64)
         nc.vector.memset(spread[:], 0.0)
 
-        spare = (WORD_BYTES * BANK, 0)
-        hid_scale_sb = [keep.tile([P, Q + spare[z]], U8, name="hid_plane%d" % z, align_bytes=64) for z in range(PASSES)]
-        zeros = hid_scale_sb[0][:, Q:]
-        nc.vector.memset(zeros.bitcast(I32), 0)
+        hid_scale_sb = [keep.tile([P, Q], U8, name="hid_plane%d" % z, align_bytes=64) for z in range(PASSES)]
 
         hid_codes = []
         for z in range(PASSES):
@@ -84,7 +88,7 @@ def tile_attend_beamvocab_kernel(tc, hid, voc_words, voc_scales, bonus, offs, ou
                 hid_rows[z][:, :, CAST_SPLIT:].rearrange("p t (c i) -> p c t i", i=LINE),
             )
             codes = keep.tile([P, Q], U32, name="hid_codes%d" % z, align_bytes=64)
-            nc.vector.quantize_mx(codes[:].bitcast(FP8X4), hid_scale_sb[z][:, :Q], grouped[:].rearrange("p q t -> p (q t)"))
+            nc.vector.quantize_mx(codes[:].bitcast(FP8X4), hid_scale_sb[z][:], grouped[:].rearrange("p q t -> p (q t)"))
             hid_codes.append(codes)
 
         logits = keep.tile([P, V], F32, name="logits")
@@ -95,13 +99,14 @@ def tile_attend_beamvocab_kernel(tc, hid, voc_words, voc_scales, bonus, offs, ou
             numbers = range(groups_before, groups_before + len(columns))
             sums = [psum.tile([P, BANK], F32, name="sums%d" % c0, tag="bank%d" % (g % BANKS)) for g, c0 in zip(numbers, columns)]
             if first == 0:
+                first_bytes = words_sb[:].rearrange("p z c -> p (z c)")
                 for warm_up in range(WARM_UPS):
                     nc.tensor.matmul_mx(
                         sums[0][:],
-                        lhsT=zeros[:, : PACK * Q].bitcast(FP8X4),
-                        lhsT_scale=zeros[:, :Q],
-                        rhs=zeros.bitcast(FP4X4),
-                        rhs_scale=voc_scale_sb[:, 0, :BANK],
+                        lhsT=hid_codes[0][:].bitcast(FP8X4),
+                        lhsT_scale=hid_scale_sb[0][:],
+                        rhs=first_bytes.bitcast(FP4X4),
+                        rhs_scale=first_bytes[:, :BANK],
                         start=True,
                         stop=True,
                     )
@@ -111,7 +116,7 @@ def tile_attend_beamvocab_kernel(tc, hid, voc_words, voc_scales, bonus, offs, ou
                     nc.tensor.matmul_mx(
                         acc[:, :n],
                         lhsT=hid_codes[z][:].bitcast(FP8X4),
-                        lhsT_scale=hid_scale_sb[z][:, :Q],
+                        lhsT_scale=hid_scale_sb[z][:],
                         rhs=words_sb[:, z, at : at + WORD_BYTES * n].bitcast(FP4X4),
                         rhs_scale=voc_scale_sb[:, z, c0 : c0 + n],
                         start=(z == 0),

@@ -58,11 +58,8 @@ def tile_attend_beamvocab_kernel(tc, hid, voc_words, voc_scales, bonus, offs, ou
 
         voc_scale_sb = keep.tile([P, PASSES, V], U8, name="voc_plane", align_bytes=64)
         scale_rows = voc_scales.bitcast(I32).rearrange("z (a r) c -> r a z c", r=SCALE_ROWS)
-        last = SCALE_ROWS - 1
-        for r in range(last):
+        for r in range(SCALE_ROWS):
             nc.sync.dma_start(voc_scale_sb[:].bitcast(I32)[r:P:QUADRANT, :, :], scale_rows[r])
-        for z in range(PASSES):
-            nc.sync.dma_start(voc_scale_sb[:].bitcast(I32)[last:P:QUADRANT, z, :], scale_rows[last][:, z, :])
         offsets = keep.tile([P, I // GROUP_ROWS], U16, name="offsets")
         nc.sync.dma_start(offsets[:], offs)
 
@@ -78,7 +75,7 @@ def tile_attend_beamvocab_kernel(tc, hid, voc_words, voc_scales, bonus, offs, ou
 
         hid_codes = []
         for z in range(PASSES):
-            grouped = keep.tile([P, Q, PACK], BF16, name="grouped%d" % z, align_bytes=64)
+            grouped = keep.tile([P, Q, PACK], BF16, name="grouped%d" % z, tag="grouped", align_bytes=64)
             nc.vector.tensor_copy(
                 grouped[:, :CAST_SPLIT, :].rearrange("p (c i) t -> p c t i", i=LINE),
                 hid_rows[z][:, :, :CAST_SPLIT].rearrange("p t (c i) -> p c t i", i=LINE),

@@ -58,15 +58,18 @@ def tile_attend_beamvocab_kernel(tc, hid, voc_words, voc_scales, bonus, offs, ou
 
         voc_scale_sb = keep.tile([P, PASSES, V], U8, name="voc_plane", align_bytes=64)
         scale_rows = voc_scales.bitcast(I32).rearrange("z (a r) c -> r a z c", r=SCALE_ROWS)
-        for r in range(SCALE_ROWS):
+        last = SCALE_ROWS - 1
+        for r in range(last):
             nc.sync.dma_start(voc_scale_sb[:].bitcast(I32)[r:P:QUADRANT, :, :], scale_rows[r])
-        offsets = keep.tile([P, I // GROUP_ROWS], U16, name="offsets")
-        nc.sync.dma_start(offsets[:], offs)
+        for z in range(PASSES):
+            nc.sync.dma_start(voc_scale_sb[:].bitcast(I32)[last:P:QUADRANT, z, :], scale_rows[last][:, z, :])
 
         for first, width in zip(starts[1:], STRETCHES[1:]):
             stretch_words.append(load_words(first, width))
         bonus_sb = keep.tile([P, I], F32, name="bonus_sb")
         nc.sync.dma_start(bonus_sb[:], bonus)
+        offsets = keep.tile([P, I // GROUP_ROWS], U16, name="offsets")
+        nc.sync.dma_start(offsets[:], offs)
 
         spread = keep.tile([P, V], F32, name="spread", align_bytes=64)
         nc.vector.memset(spread[:], 0.0)

@@ -41,35 +41,25 @@ def tile_attend_beamvocab_kernel(tc, hid, voc_words, voc_scales, bonus, offs, ou
         psum = ctx.enter_context(tc.psum_pool(name="psum", bufs=1))
 
         def load_hid(z):
-            rows_sb = keep.tile([P, PACK, Q], F32, name="hid_rows%d" % z)
+            rows_sb = keep.tile([P, PACK, Q], F32, name="hid_rows%d" % z, tag="rows%d" % z, align_bytes=64)
             nc.sync.dma_start(rows_sb[:], hid[z * K_PASS : (z + 1) * K_PASS, :].rearrange("(p t) q -> p t q", t=PACK))
             return rows_sb
 
-        def load_words(first, width):
-            words_sb = keep.tile([P, PASSES, WORD_BYTES * width], U8, name="words%d" % first, align_bytes=64)
+        def load_words(first, width, tag):
+            words_sb = keep.tile([P, PASSES, WORD_BYTES * width], U8, name="words%d" % first, tag=tag, align_bytes=64)
             words_hbm = voc_words[:, :, WORD_BYTES * first : WORD_BYTES * (first + width)].bitcast(I32)
             nc.sync.dma_start(words_sb[:].bitcast(I32), words_hbm.rearrange("z p c -> p z c"))
             return words_sb
 
         starts = [sum(STRETCHES[:k]) for k in range(len(STRETCHES))]
         hid_rows = [load_hid(0)]
-        stretch_words = [load_words(starts[0], STRETCHES[0])]
+        stretch_words = [load_words(starts[0], STRETCHES[0], "words0")]
         hid_rows.append(load_hid(1))
 
         voc_scale_sb = keep.tile([P, PASSES, V], U8, name="voc_plane", align_bytes=64)
         scale_rows = voc_scales.bitcast(I32).rearrange("z (a r) c -> r a z c", r=SCALE_ROWS)
-        last = SCALE_ROWS - 1
-        for r in range(last):
+        for r in range(SCALE_ROWS):
             nc.sync.dma_start(voc_scale_sb[:].bitcast(I32)[r:P:QUADRANT, :, :], scale_rows[r])
-        for z in range(PASSES):
-            nc.sync.dma_start(voc_scale_sb[:].bitcast(I32)[last:P:QUADRANT, z, :], scale_rows[last][:, z, :])
-
-        for first, width in zip(starts[1:], STRETCHES[1:]):
-            stretch_words.append(load_words(first, width))
-        bonus_sb = keep.tile([P, I], F32, name="bonus_sb")
-        nc.sync.dma_start(bonus_sb[:], bonus)
-        offsets = keep.tile([P, I // GROUP_ROWS], U16, name="offsets")
-        nc.sync.dma_start(offsets[:], offs)
 
         spread = keep.tile([P, V], F32, name="spread", align_bytes=64)
         nc.vector.memset(spread[:], 0.0)
@@ -90,6 +80,14 @@ def tile_attend_beamvocab_kernel(tc, hid, voc_words, voc_scales, bonus, offs, ou
             codes = keep.tile([P, Q], U32, name="hid_codes%d" % z, align_bytes=64)
             nc.vector.quantize_mx(codes[:].bitcast(FP8X4), hid_scale_sb[z][:], grouped[:].rearrange("p q t -> p (q t)"))
             hid_codes.append(codes)
+
+        tags = ["rows0"] + ["words%d" % first for first in starts[2:]]
+        for first, width, tag in zip(starts[1:], STRETCHES[1:], tags):
+            stretch_words.append(load_words(first, width, tag))
+        bonus_sb = keep.tile([P, I], F32, name="bonus_sb")
+        nc.sync.dma_start(bonus_sb[:], bonus)
+        offsets = keep.tile([P, I // GROUP_ROWS], U16, name="offsets")
+        nc.sync.dma_start(offsets[:], offs)
 
         logits = keep.tile([P, V], F32, name="logits")
         groups_before = 0

@@ -27,10 +27,8 @@ GROUP_ROWS = 16
 QUADRANT = 32
 SCALE_ROWS = 4
 BANK = 512
-BANKS = 8
-NARROW = 128
-WARM_UPS = 2
-STRETCHES = (256, 512, 512, 384, 384)
+GROUPS = (128, 128, 256, 512, 512, 256, 128, 128)
+PIECES = ((1024, 1024), (1024, 512, 512))
 CAST_SPLIT = 80
 
 
@@ -41,32 +39,40 @@ def tile_attend_beamvocab_kernel(tc, hid, voc_words, voc_scales, bonus, offs, ou
         psum = ctx.enter_context(tc.psum_pool(name="psum", bufs=1))
 
         def load_hid(z):
-            rows_sb = keep.tile([P, PACK, Q], F32, name="hid_rows%d" % z, tag="rows%d" % z, align_bytes=64)
+            rows_sb = keep.tile([P, PACK, Q], F32, name="hid_rows%d" % z, align_bytes=64)
             nc.sync.dma_start(rows_sb[:], hid[z * K_PASS : (z + 1) * K_PASS, :].rearrange("(p t) q -> p t q", t=PACK))
             return rows_sb
 
-        def load_words(first, width, tag):
-            words_sb = keep.tile([P, PASSES, WORD_BYTES * width], U8, name="words%d" % first, tag=tag, align_bytes=64)
-            words_hbm = voc_words[:, :, WORD_BYTES * first : WORD_BYTES * (first + width)].bitcast(I32)
-            nc.sync.dma_start(words_sb[:].bitcast(I32), words_hbm.rearrange("z p c -> p z c"))
-            return words_sb
+        def load_scales(z):
+            plane_sb = keep.tile([P, V], U8, name="voc_plane%d" % z, align_bytes=64)
+            rows_hbm = voc_scales[z].bitcast(I32).rearrange("(a r) c -> r a c", r=SCALE_ROWS)
+            for r in range(SCALE_ROWS):
+                nc.sync.dma_start(plane_sb[:].bitcast(I32)[r:P:QUADRANT, :], rows_hbm[r])
+            return plane_sb
 
-        starts = [sum(STRETCHES[:k]) for k in range(len(STRETCHES))]
+        def load_words(z, k):
+            first, width = sum(PIECES[z][:k]), PIECES[z][k]
+            words_sb = keep.tile([P, WORD_BYTES * width], U8, name="words%d_%d" % (z, k), align_bytes=64)
+            words_hbm = voc_words[z, :, WORD_BYTES * first : WORD_BYTES * (first + width)]
+            nc.sync.dma_start(words_sb[:].bitcast(I32), words_hbm.bitcast(I32))
+            return (first, width, words_sb)
+
+        voc_scale_sb = [load_scales(0)]
         hid_rows = [load_hid(0)]
-        stretch_words = [load_words(starts[0], STRETCHES[0], "words0")]
+        pieces = [[load_words(0, k) for k in range(len(PIECES[0]))]]
         hid_rows.append(load_hid(1))
-
-        voc_scale_sb = keep.tile([P, PASSES, V], U8, name="voc_plane", align_bytes=64)
-        scale_rows = voc_scales.bitcast(I32).rearrange("z (a r) c -> r a z c", r=SCALE_ROWS)
-        for r in range(SCALE_ROWS):
-            nc.sync.dma_start(voc_scale_sb[:].bitcast(I32)[r:P:QUADRANT, :, :], scale_rows[r])
+        voc_scale_sb.append(load_scales(1))
+        pieces.append([load_words(1, 0)])
+        offsets = keep.tile([P, I // GROUP_ROWS], U16, name="offsets")
+        nc.sync.dma_start(offsets[:], offs)
+        pieces[1].extend(load_words(1, k) for k in range(1, len(PIECES[1])))
+        bonus_sb = keep.tile([P, I], F32, name="bonus_sb")
+        nc.sync.dma_start(bonus_sb[:], bonus)
 
         spread = keep.tile([P, V], F32, name="spread", align_bytes=64)
         nc.vector.memset(spread[:], 0.0)
 
-        hid_scale_sb = [keep.tile([P, Q], U8, name="hid_plane%d" % z, align_bytes=64) for z in range(PASSES)]
-
-        hid_codes = []
+        hid_codes, hid_scale_sb = [], []
         for z in range(PASSES):
             grouped = keep.tile([P, Q, PACK], BF16, name="grouped%d" % z, tag="grouped", align_bytes=64)
             nc.vector.tensor_copy(
@@ -78,54 +84,33 @@ def tile_attend_beamvocab_kernel(tc, hid, voc_words, voc_scales, bonus, offs, ou
                 hid_rows[z][:, :, CAST_SPLIT:].rearrange("p t (c i) -> p c t i", i=LINE),
             )
             codes = keep.tile([P, Q], U32, name="hid_codes%d" % z, align_bytes=64)
-            nc.vector.quantize_mx(codes[:].bitcast(FP8X4), hid_scale_sb[z][:], grouped[:].rearrange("p q t -> p (q t)"))
+            plane = keep.tile([P, Q], U8, name="hid_plane%d" % z, align_bytes=64)
+            nc.vector.quantize_mx(codes[:].bitcast(FP8X4), plane[:], grouped[:].rearrange("p q t -> p (q t)"))
             hid_codes.append(codes)
-
-        tags = ["rows0"] + ["words%d" % first for first in starts[2:]]
-        for first, width, tag in zip(starts[1:], STRETCHES[1:], tags):
-            stretch_words.append(load_words(first, width, tag))
-        bonus_sb = keep.tile([P, I], F32, name="bonus_sb")
-        nc.sync.dma_start(bonus_sb[:], bonus)
-        offsets = keep.tile([P, I // GROUP_ROWS], U16, name="offsets")
-        nc.sync.dma_start(offsets[:], offs)
+            hid_scale_sb.append(plane)
 
         logits = keep.tile([P, V], F32, name="logits")
-        groups_before = 0
-        for first, width, words_sb in zip(starts, STRETCHES, stretch_words):
-            n = BANK if width == BANK else NARROW
-            columns = list(range(first, first + width, n))
-            numbers = range(groups_before, groups_before + len(columns))
-            sums = [psum.tile([P, BANK], F32, name="sums%d" % c0, tag="bank%d" % (g % BANKS)) for g, c0 in zip(numbers, columns)]
-            if first == 0:
-                first_bytes = words_sb[:].rearrange("p z c -> p (z c)")
-                for warm_up in range(WARM_UPS):
-                    nc.tensor.matmul_mx(
-                        sums[0][:],
-                        lhsT=hid_codes[0][:].bitcast(FP8X4),
-                        lhsT_scale=hid_scale_sb[0][:],
-                        rhs=first_bytes.bitcast(FP4X4),
-                        rhs_scale=first_bytes[:, :BANK],
-                        start=True,
-                        stop=True,
-                    )
-            for z in range(PASSES):
-                for c0, acc in zip(columns, sums):
-                    at = WORD_BYTES * (c0 - first)
-                    nc.tensor.matmul_mx(
-                        acc[:, :n],
-                        lhsT=hid_codes[z][:].bitcast(FP8X4),
-                        lhsT_scale=hid_scale_sb[z][:],
-                        rhs=words_sb[:, z, at : at + WORD_BYTES * n].bitcast(FP4X4),
-                        rhs_scale=voc_scale_sb[:, z, c0 : c0 + n],
-                        start=(z == 0),
-                        stop=(z == PASSES - 1),
-                    )
-            for g, c0, acc in zip(numbers, columns, sums):
-                if g % 2 == 1:
-                    nc.scalar.activation(logits[:, c0 : c0 + n], acc[:, :n], ACT.Copy)
-                else:
-                    nc.vector.tensor_copy(logits[:, c0 : c0 + n], acc[:, :n])
-            groups_before = groups_before + len(columns)
+        sums = [psum.tile([P, BANK], F32, name="sums%d" % g) for g in range(len(GROUPS))]
+        for z in range(PASSES):
+            for g, n in enumerate(GROUPS):
+                c0 = sum(GROUPS[:g])
+                first, words_sb = [(f, w) for f, width, w in pieces[z] if f <= c0 < f + width][0]
+                at = WORD_BYTES * (c0 - first)
+                nc.tensor.matmul_mx(
+                    sums[g][:, :n],
+                    lhsT=hid_codes[z][:].bitcast(FP8X4),
+                    lhsT_scale=hid_scale_sb[z][:],
+                    rhs=words_sb[:, at : at + WORD_BYTES * n].bitcast(FP4X4),
+                    rhs_scale=voc_scale_sb[z][:, c0 : c0 + n],
+                    start=(z == 0),
+                    stop=(z == PASSES - 1),
+                )
+        for g, n in enumerate(GROUPS):
+            c0 = sum(GROUPS[:g])
+            if g % 2 == 1:
+                nc.scalar.activation(logits[:, c0 : c0 + n], sums[g][:, :n], ACT.Copy)
+            else:
+                nc.vector.tensor_copy(logits[:, c0 : c0 + n], sums[g][:, :n])
 
         scores = keep.tile([P, I], F32, name="scores")
         nc.vector.tensor_tensor(scores[:], logits[:].indirect(offsets[:]), bonus_sb[:], ALU.add)

@@ -27,8 +27,9 @@ GROUP_ROWS = 16
 QUADRANT = 32
 SCALE_ROWS = 4
 BANK = 512
-GROUPS = (128, 128, 256, 512, 512, 256, 128, 128)
-PIECES = ((1024, 1024), (1024, 512, 512))
+BANKS = 8
+GROUP = V // BANKS
+PIECES = ((1024, 512, 512), (1024, 1024))
 CAST_SPLIT = 80
 
 
@@ -39,78 +40,78 @@ def tile_attend_beamvocab_kernel(tc, hid, voc_words, voc_scales, bonus, offs, ou
         psum = ctx.enter_context(tc.psum_pool(name="psum", bufs=1))
 
         def load_hid(z):
-            rows_sb = keep.tile([P, PACK, Q], F32, name="hid_rows%d" % z, align_bytes=64)
+            rows_sb = keep.tile([P, PACK, Q], F32, name="hid_rows%d" % z, tag="rows%d" % z, align_bytes=64)
             nc.sync.dma_start(rows_sb[:], hid[z * K_PASS : (z + 1) * K_PASS, :].rearrange("(p t) q -> p t q", t=PACK))
             return rows_sb
 
-        def load_scales(z):
-            plane_sb = keep.tile([P, V], U8, name="voc_plane%d" % z, align_bytes=64)
-            rows_hbm = voc_scales[z].bitcast(I32).rearrange("(a r) c -> r a c", r=SCALE_ROWS)
-            for r in range(SCALE_ROWS):
-                nc.sync.dma_start(plane_sb[:].bitcast(I32)[r:P:QUADRANT, :], rows_hbm[r])
-            return plane_sb
-
-        def load_words(z, k):
+        def load_words(z, k, tag):
             first, width = sum(PIECES[z][:k]), PIECES[z][k]
-            words_sb = keep.tile([P, WORD_BYTES * width], U8, name="words%d_%d" % (z, k), align_bytes=64)
+            words_sb = keep.tile([P, WORD_BYTES * width], U8, name="words%d_%d" % (z, k), tag=tag, align_bytes=64)
             words_hbm = voc_words[z, :, WORD_BYTES * first : WORD_BYTES * (first + width)]
             nc.sync.dma_start(words_sb[:].bitcast(I32), words_hbm.bitcast(I32))
             return (first, width, words_sb)
 
-        voc_scale_sb = [load_scales(0)]
-        hid_rows = [load_hid(0)]
-        pieces = [[load_words(0, k) for k in range(len(PIECES[0]))]]
-        hid_rows.append(load_hid(1))
-        voc_scale_sb.append(load_scales(1))
-        pieces.append([load_words(1, 0)])
-        offsets = keep.tile([P, I // GROUP_ROWS], U16, name="offsets")
-        nc.sync.dma_start(offsets[:], offs)
-        pieces[1].extend(load_words(1, k) for k in range(1, len(PIECES[1])))
-        bonus_sb = keep.tile([P, I], F32, name="bonus_sb")
-        nc.sync.dma_start(bonus_sb[:], bonus)
-
-        spread = keep.tile([P, V], F32, name="spread", align_bytes=64)
-        nc.vector.memset(spread[:], 0.0)
-
-        hid_codes, hid_scale_sb = [], []
-        for z in range(PASSES):
-            grouped = keep.tile([P, Q, PACK], BF16, name="grouped%d" % z, tag="grouped", align_bytes=64)
+        def quantise_hid(z, rows_sb):
+            grouped = keep.tile([P, Q, PACK], BF16, name="grouped%d" % z, align_bytes=64)
             nc.vector.tensor_copy(
                 grouped[:, :CAST_SPLIT, :].rearrange("p (c i) t -> p c t i", i=LINE),
-                hid_rows[z][:, :, :CAST_SPLIT].rearrange("p t (c i) -> p c t i", i=LINE),
+                rows_sb[:, :, :CAST_SPLIT].rearrange("p t (c i) -> p c t i", i=LINE),
             )
             nc.scalar.copy(
                 grouped[:, CAST_SPLIT:, :].rearrange("p (c i) t -> p c t i", i=LINE),
-                hid_rows[z][:, :, CAST_SPLIT:].rearrange("p t (c i) -> p c t i", i=LINE),
+                rows_sb[:, :, CAST_SPLIT:].rearrange("p t (c i) -> p c t i", i=LINE),
             )
             codes = keep.tile([P, Q], U32, name="hid_codes%d" % z, align_bytes=64)
             plane = keep.tile([P, Q], U8, name="hid_plane%d" % z, align_bytes=64)
             nc.vector.quantize_mx(codes[:].bitcast(FP8X4), plane[:], grouped[:].rearrange("p q t -> p (q t)"))
-            hid_codes.append(codes)
-            hid_scale_sb.append(plane)
+            return (codes, plane)
+
+        first_rows = load_hid(0)
+        pieces = [[load_words(0, 0, "words0_0")]]
+
+        voc_scale_sb = keep.tile([P, PASSES, V], U8, name="voc_plane", align_bytes=64)
+        scale_rows = voc_scales.bitcast(I32).rearrange("z (a r) c -> r a z c", r=SCALE_ROWS)
+        for r in range(SCALE_ROWS):
+            nc.sync.dma_start(voc_scale_sb[:].bitcast(I32)[r:P:QUADRANT, :, :], scale_rows[r])
+
+        spread = keep.tile([P, V], F32, name="spread", align_bytes=64)
+        nc.vector.memset(spread[:], 0.0)
+
+        hid_mx = [quantise_hid(0, first_rows)]
+
+        pieces[0].append(load_words(0, 1, "rows0"))
+        second_rows = load_hid(1)
+        pieces[0].append(load_words(0, 2, "words0_2"))
+        pieces.append([load_words(1, k, "words1_%d" % k) for k in range(len(PIECES[1]))])
+        bonus_sb = keep.tile([P, I], F32, name="bonus_sb")
+        nc.sync.dma_start(bonus_sb[:], bonus)
+        offsets = keep.tile([P, I // GROUP_ROWS], U16, name="offsets")
+        nc.sync.dma_start(offsets[:], offs)
+        hid_mx.append(quantise_hid(1, second_rows))
 
         logits = keep.tile([P, V], F32, name="logits")
-        sums = [psum.tile([P, BANK], F32, name="sums%d" % g) for g in range(len(GROUPS))]
+        sums = [psum.tile([P, BANK], F32, name="sums%d" % g) for g in range(BANKS)]
         for z in range(PASSES):
-            for g, n in enumerate(GROUPS):
-                c0 = sum(GROUPS[:g])
+            codes, plane = hid_mx[z]
+            for g in range(BANKS):
+                c0 = g * GROUP
                 first, words_sb = [(f, w) for f, width, w in pieces[z] if f <= c0 < f + width][0]
                 at = WORD_BYTES * (c0 - first)
                 nc.tensor.matmul_mx(
-                    sums[g][:, :n],
-                    lhsT=hid_codes[z][:].bitcast(FP8X4),
-                    lhsT_scale=hid_scale_sb[z][:],
-                    rhs=words_sb[:, at : at + WORD_BYTES * n].bitcast(FP4X4),
-                    rhs_scale=voc_scale_sb[z][:, c0 : c0 + n],
+                    sums[g][:, :GROUP],
+                    lhsT=codes[:].bitcast(FP8X4),
+                    lhsT_scale=plane[:],
+                    rhs=words_sb[:, at : at + WORD_BYTES * GROUP].bitcast(FP4X4),
+                    rhs_scale=voc_scale_sb[:, z, c0 : c0 + GROUP],
                     start=(z == 0),
                     stop=(z == PASSES - 1),
                 )
-        for g, n in enumerate(GROUPS):
-            c0 = sum(GROUPS[:g])
+        for g in range(BANKS):
+            c0 = g * GROUP
             if g % 2 == 1:
-                nc.scalar.activation(logits[:, c0 : c0 + n], sums[g][:, :n], ACT.Copy)
+                nc.scalar.activation(logits[:, c0 : c0 + GROUP], sums[g][:, :GROUP], ACT.Copy)
             else:
-                nc.vector.tensor_copy(logits[:, c0 : c0 + n], sums[g][:, :n])
+                nc.vector.tensor_copy(logits[:, c0 : c0 + GROUP], sums[g][:, :GROUP])
 
         scores = keep.tile([P, I], F32, name="scores")
         nc.vector.tensor_tensor(scores[:], logits[:].indirect(offsets[:]), bonus_sb[:], ALU.add)

@@ -30,6 +30,7 @@ BANK = 512
 BANKS = 8
 GROUP = V // BANKS
 PIECES = ((1024, 512, 512), (1024, 1024))
+WARM_UPS = (256, 128)
 CAST_SPLIT = 80
 
 
@@ -91,6 +92,17 @@ def tile_attend_beamvocab_kernel(tc, hid, voc_words, voc_scales, bonus, offs, ou
 
         logits = keep.tile([P, V], F32, name="logits")
         sums = [psum.tile([P, BANK], F32, name="sums%d" % g) for g in range(BANKS)]
+        first_bytes = pieces[0][0][2]
+        for n in WARM_UPS:
+            nc.tensor.matmul_mx(
+                sums[0][:, :n],
+                lhsT=hid_mx[0][0][:].bitcast(FP8X4),
+                lhsT_scale=hid_mx[0][1][:],
+                rhs=first_bytes[:, : WORD_BYTES * n].bitcast(FP4X4),
+                rhs_scale=first_bytes[:, :n],
+                start=True,
+                stop=True,
+            )
         for z in range(PASSES):
             codes, plane = hid_mx[z]
             for g in range(BANKS):

@@ -29,7 +29,7 @@ SCALE_ROWS = 4
 BANK = 512
 BANKS = 8
 GROUP = V // BANKS
-PIECES = ((1024, 512, 512), (1024, 1024))
+PIECES = ((1024, 1024), (768, 768, 512))
 WARM_UPS = (256, 128)
 CAST_SPLIT = 80
 
@@ -41,13 +41,13 @@ def tile_attend_beamvocab_kernel(tc, hid, voc_words, voc_scales, bonus, offs, ou
         psum = ctx.enter_context(tc.psum_pool(name="psum", bufs=1))
 
         def load_hid(z):
-            rows_sb = keep.tile([P, PACK, Q], F32, name="hid_rows%d" % z, tag="rows%d" % z, align_bytes=64)
+            rows_sb = keep.tile([P, PACK, Q], F32, name="hid_rows%d" % z, tag="rows", align_bytes=64)
             nc.sync.dma_start(rows_sb[:], hid[z * K_PASS : (z + 1) * K_PASS, :].rearrange("(p t) q -> p t q", t=PACK))
             return rows_sb
 
-        def load_words(z, k, tag):
+        def load_words(z, k):
             first, width = sum(PIECES[z][:k]), PIECES[z][k]
-            words_sb = keep.tile([P, WORD_BYTES * width], U8, name="words%d_%d" % (z, k), tag=tag, align_bytes=64)
+            words_sb = keep.tile([P, WORD_BYTES * width], U8, name="words%d_%d" % (z, k), align_bytes=64)
             words_hbm = voc_words[z, :, WORD_BYTES * first : WORD_BYTES * (first + width)]
             nc.sync.dma_start(words_sb[:].bitcast(I32), words_hbm.bitcast(I32))
             return (first, width, words_sb)
@@ -68,7 +68,7 @@ def tile_attend_beamvocab_kernel(tc, hid, voc_words, voc_scales, bonus, offs, ou
             return (codes, plane)
 
         first_rows = load_hid(0)
-        pieces = [[load_words(0, 0, "words0_0")]]
+        pieces = [[load_words(0, 0)]]
 
         voc_scale_sb = keep.tile([P, PASSES, V], U8, name="voc_plane", align_bytes=64)
         scale_rows = voc_scales.bitcast(I32).rearrange("z (a r) c -> r a z c", r=SCALE_ROWS)
@@ -80,10 +80,9 @@ def tile_attend_beamvocab_kernel(tc, hid, voc_words, voc_scales, bonus, offs, ou
 
         hid_mx = [quantise_hid(0, first_rows)]
 
-        pieces[0].append(load_words(0, 1, "rows0"))
         second_rows = load_hid(1)
-        pieces[0].append(load_words(0, 2, "words0_2"))
-        pieces.append([load_words(1, k, "words1_%d" % k) for k in range(len(PIECES[1]))])
+        pieces[0].append(load_words(0, 1))
+        pieces.append([load_words(1, k) for k in range(len(PIECES[1]))])
         bonus_sb = keep.tile([P, I], F32, name="bonus_sb")
         nc.sync.dma_start(bonus_sb[:], bonus)
         offsets = keep.tile([P, I // GROUP_ROWS], U16, name="offsets")

@@ -28,8 +28,11 @@ QUADRANT = 32
 SCALE_ROWS = 4
 BANK = 512
 BANKS = 8
-GROUP = V // BANKS
-PIECES = ((1024, 1024), (768, 768, 512))
+GROUP = 256
+NARROW = 128
+EARLY_PIECES = ((1024, 512), (768, 768))
+EARLY = sum(EARLY_PIECES[0])
+LATE_PIECE = 256
 WARM_UPS = (256, 128)
 CAST_SPLIT = 80
 
@@ -45,12 +48,15 @@ def tile_attend_beamvocab_kernel(tc, hid, voc_words, voc_scales, bonus, offs, ou
             nc.sync.dma_start(rows_sb[:], hid[z * K_PASS : (z + 1) * K_PASS, :].rearrange("(p t) q -> p t q", t=PACK))
             return rows_sb
 
-        def load_words(z, k):
-            first, width = sum(PIECES[z][:k]), PIECES[z][k]
-            words_sb = keep.tile([P, WORD_BYTES * width], U8, name="words%d_%d" % (z, k), align_bytes=64)
-            words_hbm = voc_words[z, :, WORD_BYTES * first : WORD_BYTES * (first + width)]
-            nc.sync.dma_start(words_sb[:].bitcast(I32), words_hbm.bitcast(I32))
-            return (first, width, words_sb)
+        def load_words(passes, first, width):
+            words_sb = keep.tile([P, len(passes), WORD_BYTES * width], U8, name="words%d_%d" % (passes[0], first), align_bytes=64)
+            words_hbm = voc_words[passes[0] : passes[-1] + 1, :, WORD_BYTES * first : WORD_BYTES * (first + width)]
+            nc.sync.dma_start(words_sb[:].bitcast(I32), words_hbm.bitcast(I32).rearrange("z p c -> p z c"))
+            for k, z in enumerate(passes):
+                word_rows[z].append((first, width, words_sb[:, k, :]))
+
+        def load_early(z, k):
+            load_words([z], sum(EARLY_PIECES[z][:k]), EARLY_PIECES[z][k])
 
         def quantise_hid(z, rows_sb):
             grouped = keep.tile([P, Q, PACK], BF16, name="grouped%d" % z, align_bytes=64)
@@ -68,7 +74,8 @@ def tile_attend_beamvocab_kernel(tc, hid, voc_words, voc_scales, bonus, offs, ou
             return (codes, plane)
 
         first_rows = load_hid(0)
-        pieces = [[load_words(0, 0)]]
+        word_rows = [[] for z in range(PASSES)]
+        load_early(0, 0)
 
         voc_scale_sb = keep.tile([P, PASSES, V], U8, name="voc_plane", align_bytes=64)
         scale_rows = voc_scales.bitcast(I32).rearrange("z (a r) c -> r a z c", r=SCALE_ROWS)
@@ -81,8 +88,11 @@ def tile_attend_beamvocab_kernel(tc, hid, voc_words, voc_scales, bonus, offs, ou
         hid_mx = [quantise_hid(0, first_rows)]
 
         second_rows = load_hid(1)
-        pieces[0].append(load_words(0, 1))
-        pieces.append([load_words(1, k) for k in range(len(PIECES[1]))])
+        load_early(0, 1)
+        for k in range(len(EARLY_PIECES[1])):
+            load_early(1, k)
+        for first in range(EARLY, V, LATE_PIECE):
+            load_words(list(range(PASSES)), first, LATE_PIECE)
         bonus_sb = keep.tile([P, I], F32, name="bonus_sb")
         nc.sync.dma_start(bonus_sb[:], bonus)
         offsets = keep.tile([P, I // GROUP_ROWS], U16, name="offsets")
@@ -90,11 +100,41 @@ def tile_attend_beamvocab_kernel(tc, hid, voc_words, voc_scales, bonus, offs, ou
         hid_mx.append(quantise_hid(1, second_rows))
 
         logits = keep.tile([P, V], F32, name="logits")
-        sums = [psum.tile([P, BANK], F32, name="sums%d" % g) for g in range(BANKS)]
-        first_bytes = pieces[0][0][2]
+        widths = [GROUP] * (V // GROUP - 1) + [NARROW] * (GROUP // NARROW)
+        starts = [sum(widths[:g]) for g in range(len(widths))]
+        early_groups = EARLY // GROUP
+
+        def open_group(g):
+            return psum.tile([P, BANK], F32, name="sums%d" % g, tag="bank%d" % (g % BANKS))
+
+        def one_pass(g, z, sums):
+            c0, n = starts[g], widths[g]
+            codes, plane = hid_mx[z]
+            first, row = [(f, r) for f, width, r in word_rows[z] if f <= c0 < f + width][0]
+            at = WORD_BYTES * (c0 - first)
+            nc.tensor.matmul_mx(
+                sums[:, :n],
+                lhsT=codes[:].bitcast(FP8X4),
+                lhsT_scale=plane[:],
+                rhs=row[:, at : at + WORD_BYTES * n].bitcast(FP4X4),
+                rhs_scale=voc_scale_sb[:, z, c0 : c0 + n],
+                start=(z == 0),
+                stop=(z == PASSES - 1),
+            )
+
+        def copy_out(g, sums):
+            c0, n = starts[g], widths[g]
+            if (len(widths) - g) % 2 == 1:
+                nc.scalar.activation(logits[:, c0 : c0 + n], sums[:, :n], ACT.Copy)
+            else:
+                nc.vector.tensor_copy(logits[:, c0 : c0 + n], sums[:, :n])
+
+        early_sums = [open_group(g) for g in range(early_groups)]
+
+        first_bytes = word_rows[0][0][2]
         for n in WARM_UPS:
             nc.tensor.matmul_mx(
-                sums[0][:, :n],
+                early_sums[0][:, :n],
                 lhsT=hid_mx[0][0][:].bitcast(FP8X4),
                 lhsT_scale=hid_mx[0][1][:],
                 rhs=first_bytes[:, : WORD_BYTES * n].bitcast(FP4X4),
@@ -103,26 +143,15 @@ def tile_attend_beamvocab_kernel(tc, hid, voc_words, voc_scales, bonus, offs, ou
                 stop=True,
             )
         for z in range(PASSES):
-            codes, plane = hid_mx[z]
-            for g in range(BANKS):
-                c0 = g * GROUP
-                first, words_sb = [(f, w) for f, width, w in pieces[z] if f <= c0 < f + width][0]
-                at = WORD_BYTES * (c0 - first)
-                nc.tensor.matmul_mx(
-                    sums[g][:, :GROUP],
-                    lhsT=codes[:].bitcast(FP8X4),
-                    lhsT_scale=plane[:],
-                    rhs=words_sb[:, at : at + WORD_BYTES * GROUP].bitcast(FP4X4),
-                    rhs_scale=voc_scale_sb[:, z, c0 : c0 + GROUP],
-                    start=(z == 0),
-                    stop=(z == PASSES - 1),
-                )
-        for g in range(BANKS):
-            c0 = g * GROUP
-            if g % 2 == 1:
-                nc.scalar.activation(logits[:, c0 : c0 + GROUP], sums[g][:, :GROUP], ACT.Copy)
-            else:
-                nc.vector.tensor_copy(logits[:, c0 : c0 + GROUP], sums[g][:, :GROUP])
+            for g in range(early_groups):
+                one_pass(g, z, early_sums[g])
+        for g in range(early_groups):
+            copy_out(g, early_sums[g])
+        for g in range(early_groups, len(widths)):
+            sums = open_group(g)
+            for z in range(PASSES):
+                one_pass(g, z, sums)
+            copy_out(g, sums)
 
         scores = keep.tile([P, I], F32, name="scores")
         nc.vector.tensor_tensor(scores[:], logits[:].indirect(offsets[:]), bonus_sb[:], ALU.add)

@@ -30,9 +30,10 @@ BANK = 512
 BANKS = 8
 GROUP = 256
 NARROW = 128
-EARLY_PIECES = ((1024, 512), (768, 768))
+EARLY_PIECES = ((768, 512), (768, 512))
 EARLY = sum(EARLY_PIECES[0])
-LATE_PIECE = 256
+LATE_PIECES = (512, 256)
+WHOLE_SCALE_ROWS = 2
 WARM_UPS = (256, 128)
 CAST_SPLIT = 80
 
@@ -44,7 +45,7 @@ def tile_attend_beamvocab_kernel(tc, hid, voc_words, voc_scales, bonus, offs, ou
         psum = ctx.enter_context(tc.psum_pool(name="psum", bufs=1))
 
         def load_hid(z):
-            rows_sb = keep.tile([P, PACK, Q], F32, name="hid_rows%d" % z, tag="rows", align_bytes=64)
+            rows_sb = keep.tile([P, PACK, Q], F32, name="hid_rows%d" % z, align_bytes=64)
             nc.sync.dma_start(rows_sb[:], hid[z * K_PASS : (z + 1) * K_PASS, :].rearrange("(p t) q -> p t q", t=PACK))
             return rows_sb
 
@@ -80,7 +81,9 @@ def tile_attend_beamvocab_kernel(tc, hid, voc_words, voc_scales, bonus, offs, ou
         voc_scale_sb = keep.tile([P, PASSES, V], U8, name="voc_plane", align_bytes=64)
         scale_rows = voc_scales.bitcast(I32).rearrange("z (a r) c -> r a z c", r=SCALE_ROWS)
         for r in range(SCALE_ROWS):
-            nc.sync.dma_start(voc_scale_sb[:].bitcast(I32)[r:P:QUADRANT, :, :], scale_rows[r])
+            step = PASSES if r < WHOLE_SCALE_ROWS else 1
+            for z in range(0, PASSES, step):
+                nc.sync.dma_start(voc_scale_sb[:].bitcast(I32)[r:P:QUADRANT, z : z + step, :], scale_rows[r][:, z : z + step, :])
 
         spread = keep.tile([P, V], F32, name="spread", align_bytes=64)
         nc.vector.memset(spread[:], 0.0)
@@ -91,8 +94,8 @@ def tile_attend_beamvocab_kernel(tc, hid, voc_words, voc_scales, bonus, offs, ou
         load_early(0, 1)
         for k in range(len(EARLY_PIECES[1])):
             load_early(1, k)
-        for first in range(EARLY, V, LATE_PIECE):
-            load_words(list(range(PASSES)), first, LATE_PIECE)
+        for k, width in enumerate(LATE_PIECES):
+            load_words(list(range(PASSES)), EARLY + sum(LATE_PIECES[:k]), width)
         bonus_sb = keep.tile([P, I], F32, name="bonus_sb")
         nc.sync.dma_start(bonus_sb[:], bonus)
         offsets = keep.tile([P, I // GROUP_ROWS], U16, name="offsets")

@@ -30,10 +30,9 @@ BANK = 512
 BANKS = 8
 GROUP = 256
 NARROW = 128
-EARLY_PIECES = ((768, 512), (768, 512))
+EARLY_PIECES = ((256, 256, 512, 512), (768, 768))
 EARLY = sum(EARLY_PIECES[0])
-LATE_PIECES = (512, 256)
-WHOLE_SCALE_ROWS = 2
+LATE_PIECES = (512,)
 WARM_UPS = (256, 128)
 CAST_SPLIT = 80
 
@@ -77,29 +76,29 @@ def tile_attend_beamvocab_kernel(tc, hid, voc_words, voc_scales, bonus, offs, ou
         first_rows = load_hid(0)
         word_rows = [[] for z in range(PASSES)]
         load_early(0, 0)
+        load_early(0, 1)
 
         voc_scale_sb = keep.tile([P, PASSES, V], U8, name="voc_plane", align_bytes=64)
         scale_rows = voc_scales.bitcast(I32).rearrange("z (a r) c -> r a z c", r=SCALE_ROWS)
         for r in range(SCALE_ROWS):
-            step = PASSES if r < WHOLE_SCALE_ROWS else 1
-            for z in range(0, PASSES, step):
-                nc.sync.dma_start(voc_scale_sb[:].bitcast(I32)[r:P:QUADRANT, z : z + step, :], scale_rows[r][:, z : z + step, :])
+            nc.sync.dma_start(voc_scale_sb[:].bitcast(I32)[r:P:QUADRANT, :, :], scale_rows[r])
+        offsets = keep.tile([P, I // GROUP_ROWS], U16, name="offsets")
+        nc.sync.dma_start(offsets[:], offs)
 
         spread = keep.tile([P, V], F32, name="spread", align_bytes=64)
         nc.vector.memset(spread[:], 0.0)
 
         hid_mx = [quantise_hid(0, first_rows)]
 
+        load_early(0, 2)
         second_rows = load_hid(1)
-        load_early(0, 1)
+        load_early(0, 3)
         for k in range(len(EARLY_PIECES[1])):
             load_early(1, k)
         for k, width in enumerate(LATE_PIECES):
             load_words(list(range(PASSES)), EARLY + sum(LATE_PIECES[:k]), width)
         bonus_sb = keep.tile([P, I], F32, name="bonus_sb")
         nc.sync.dma_start(bonus_sb[:], bonus)
-        offsets = keep.tile([P, I // GROUP_ROWS], U16, name="offsets")
-        nc.sync.dma_start(offsets[:], offs)
         hid_mx.append(quantise_hid(1, second_rows))
 
         logits = keep.tile([P, V], F32, name="logits")

@@ -34,7 +34,8 @@ EARLY_PIECES = ((256, 256, 512, 512), (768, 768))
 EARLY = sum(EARLY_PIECES[0])
 LATE_PIECES = (512,)
 WARM_UPS = (256, 128)
-CAST_SPLIT = 80
+CAST_SPLIT = 96
+HALF = Q // 2
 
 
 def tile_attend_beamvocab_kernel(tc, hid, voc_words, voc_scales, bonus, offs, out):
@@ -60,17 +61,23 @@ def tile_attend_beamvocab_kernel(tc, hid, voc_words, voc_scales, bonus, offs, ou
 
         def quantise_hid(z, rows_sb):
             grouped = keep.tile([P, Q, PACK], BF16, name="grouped%d" % z, align_bytes=64)
-            nc.vector.tensor_copy(
-                grouped[:, :CAST_SPLIT, :].rearrange("p (c i) t -> p c t i", i=LINE),
-                rows_sb[:, :, :CAST_SPLIT].rearrange("p t (c i) -> p c t i", i=LINE),
-            )
-            nc.scalar.copy(
-                grouped[:, CAST_SPLIT:, :].rearrange("p (c i) t -> p c t i", i=LINE),
-                rows_sb[:, :, CAST_SPLIT:].rearrange("p t (c i) -> p c t i", i=LINE),
-            )
             codes = keep.tile([P, Q], U32, name="hid_codes%d" % z, align_bytes=64)
             plane = keep.tile([P, Q], U8, name="hid_plane%d" % z, align_bytes=64)
-            nc.vector.quantize_mx(codes[:].bitcast(FP8X4), plane[:], grouped[:].rearrange("p q t -> p (q t)"))
+            for copy, c0, c1 in (
+                (nc.vector.tensor_copy, 0, HALF),
+                (nc.vector.tensor_copy, HALF, CAST_SPLIT),
+                (nc.scalar.copy, CAST_SPLIT, Q),
+            ):
+                copy(
+                    grouped[:, c0:c1, :].rearrange("p (c i) t -> p c t i", i=LINE),
+                    rows_sb[:, :, c0:c1].rearrange("p t (c i) -> p c t i", i=LINE),
+                )
+            for c0 in (0, HALF):
+                nc.vector.quantize_mx(
+                    codes[:, c0 : c0 + HALF].bitcast(FP8X4),
+                    plane[:, c0 : c0 + HALF],
+                    grouped[:, c0 : c0 + HALF, :].rearrange("p q t -> p (q t)"),
+                )
             return (codes, plane)
 
         first_rows = load_hid(0)

@@ -45,12 +45,12 @@ def tile_attend_beamvocab_kernel(tc, hid, voc_words, voc_scales, bonus, offs, ou
         psum = ctx.enter_context(tc.psum_pool(name="psum", bufs=1))
 
         def load_hid(z):
-            rows_sb = keep.tile([P, PACK, Q], F32, name="hid_rows%d" % z, align_bytes=64)
+            rows_sb = keep.tile([P, PACK, Q], F32, name="hid_rows%d" % z, align_bytes=256)
             nc.sync.dma_start(rows_sb[:], hid[z * K_PASS : (z + 1) * K_PASS, :].rearrange("(p t) q -> p t q", t=PACK))
             return rows_sb
 
         def load_words(passes, first, width):
-            words_sb = keep.tile([P, len(passes), WORD_BYTES * width], U8, name="words%d_%d" % (passes[0], first), align_bytes=64)
+            words_sb = keep.tile([P, len(passes), WORD_BYTES * width], U8, name="words%d_%d" % (passes[0], first), align_bytes=256)
             words_hbm = voc_words[passes[0] : passes[-1] + 1, :, WORD_BYTES * first : WORD_BYTES * (first + width)]
             nc.sync.dma_start(words_sb[:].bitcast(I32), words_hbm.bitcast(I32).rearrange("z p c -> p z c"))
             for k, z in enumerate(passes):
@@ -60,9 +60,9 @@ def tile_attend_beamvocab_kernel(tc, hid, voc_words, voc_scales, bonus, offs, ou
             load_words([z], sum(EARLY_PIECES[z][:k]), EARLY_PIECES[z][k])
 
         def quantise_hid(z, rows_sb):
-            grouped = keep.tile([P, Q, PACK], BF16, name="grouped%d" % z, align_bytes=64)
-            codes = keep.tile([P, Q], U32, name="hid_codes%d" % z, align_bytes=64)
-            plane = keep.tile([P, Q], U8, name="hid_plane%d" % z, align_bytes=64)
+            grouped = keep.tile([P, Q, PACK], BF16, name="grouped%d" % z, align_bytes=256)
+            codes = keep.tile([P, Q], U32, name="hid_codes%d" % z, align_bytes=256)
+            plane = keep.tile([P, Q], U8, name="hid_plane%d" % z, align_bytes=256)
             for copy, c0, c1 in (
                 (nc.vector.tensor_copy, 0, HALF),
                 (nc.vector.tensor_copy, HALF, CAST_SPLIT),
@@ -85,14 +85,14 @@ def tile_attend_beamvocab_kernel(tc, hid, voc_words, voc_scales, bonus, offs, ou
         load_early(0, 0)
         load_early(0, 1)
 
-        voc_scale_sb = keep.tile([P, PASSES, V], U8, name="voc_plane", align_bytes=64)
+        voc_scale_sb = keep.tile([P, PASSES, V], U8, name="voc_plane", align_bytes=256)
         scale_rows = voc_scales.bitcast(I32).rearrange("z (a r) c -> r a z c", r=SCALE_ROWS)
         for r in range(SCALE_ROWS):
             nc.sync.dma_start(voc_scale_sb[:].bitcast(I32)[r:P:QUADRANT, :, :], scale_rows[r])
         offsets = keep.tile([P, I // GROUP_ROWS], U16, name="offsets")
         nc.sync.dma_start(offsets[:], offs)
 
-        spread = keep.tile([P, V], F32, name="spread", align_bytes=64)
+        spread = keep.tile([P, V], F32, name="spread", align_bytes=256)
         nc.vector.memset(spread[:], 0.0)
 
         hid_mx = [quantise_hid(0, first_rows)]

@@ -89,7 +89,7 @@ def tile_attend_beamvocab_kernel(tc, hid, voc_words, voc_scales, bonus, offs, ou
         scale_rows = voc_scales.bitcast(I32).rearrange("z (a r) c -> r a z c", r=SCALE_ROWS)
         for r in range(SCALE_ROWS):
             nc.sync.dma_start(voc_scale_sb[:].bitcast(I32)[r:P:QUADRANT, :, :], scale_rows[r])
-        offsets = keep.tile([P, I // GROUP_ROWS], U16, name="offsets")
+        offsets = keep.tile([P, I // GROUP_ROWS], U16, name="offsets", align_bytes=256)
         nc.sync.dma_start(offsets[:], offs)
 
         spread = keep.tile([P, V], F32, name="spread", align_bytes=256)
@@ -104,11 +104,11 @@ def tile_attend_beamvocab_kernel(tc, hid, voc_words, voc_scales, bonus, offs, ou
             load_early(1, k)
         for k, width in enumerate(LATE_PIECES):
             load_words(list(range(PASSES)), EARLY + sum(LATE_PIECES[:k]), width)
-        bonus_sb = keep.tile([P, I], F32, name="bonus_sb")
+        bonus_sb = keep.tile([P, I], F32, name="bonus_sb", align_bytes=256)
         nc.sync.dma_start(bonus_sb[:], bonus)
         hid_mx.append(quantise_hid(1, second_rows))
 
-        logits = keep.tile([P, V], F32, name="logits")
+        logits = keep.tile([P, V], F32, name="logits", align_bytes=256)
         widths = [GROUP] * (V // GROUP - 1) + [NARROW] * (GROUP // NARROW)
         starts = [sum(widths[:g]) for g in range(len(widths))]
         early_groups = EARLY // GROUP
@@ -162,18 +162,18 @@ def tile_attend_beamvocab_kernel(tc, hid, voc_words, voc_scales, bonus, offs, ou
                 one_pass(g, z, sums)
             copy_out(g, sums)
 
-        scores = keep.tile([P, I], F32, name="scores")
+        scores = keep.tile([P, I], F32, name="scores", align_bytes=256)
         nc.vector.tensor_tensor(scores[:], logits[:].indirect(offsets[:]), bonus_sb[:], ALU.add)
 
         neg_max = keep.tile([P, 1], F32, name="neg_max")
         nc.vector.tensor_reduce(neg_max[:], scores[:], AX.X, ALU.max, negate=True)
-        exps = keep.tile([P, I], F32, name="exps")
+        exps = keep.tile([P, I], F32, name="exps", align_bytes=256)
         total = keep.tile([P, 1], F32, name="total")
         nc.scalar.activation(exps[:], scores[:], ACT.Exp, bias=neg_max[:], accum_out=total[:])
 
         inv_total = keep.tile([P, 1], F32, name="inv_total")
         nc.vector.reciprocal(inv_total[:], total[:])
-        weights = keep.tile([P, I], F32, name="weights")
+        weights = keep.tile([P, I], F32, name="weights", align_bytes=256)
         nc.vector.tensor_scalar(weights[:], exps[:], inv_total[:], float(I), ALU.mult, ALU.mult)
         nc.vector.tensor_copy(spread[:].indirect(offsets[:]), weights[:])
         nc.sync.dma_start(out, spread[:])

@@ -36,6 +36,8 @@ LATE_PIECES = (512,)
 WARM_UPS = (256, 128)
 CAST_SPLIT = 96
 HALF = Q // 2
+CODES_AT = 32
+PLANE_AT = 64
 
 
 def tile_attend_beamvocab_kernel(tc, hid, voc_words, voc_scales, bonus, offs, out):
@@ -61,8 +63,8 @@ def tile_attend_beamvocab_kernel(tc, hid, voc_words, voc_scales, bonus, offs, ou
 
         def quantise_hid(z, rows_sb):
             grouped = keep.tile([P, Q, PACK], BF16, name="grouped%d" % z, align_bytes=256)
-            codes = keep.tile([P, Q], U32, name="hid_codes%d" % z, align_bytes=256)
-            plane = keep.tile([P, Q], U8, name="hid_plane%d" % z, align_bytes=256)
+            codes = keep.tile([P, CODES_AT + Q], U32, name="hid_codes%d" % z, align_bytes=256)[:, CODES_AT:]
+            plane = keep.tile([P, PLANE_AT + Q], U8, name="hid_plane%d" % z, align_bytes=256)[:, PLANE_AT:]
             for copy, c0, c1 in (
                 (nc.vector.tensor_copy, 0, HALF),
                 (nc.vector.tensor_copy, HALF, CAST_SPLIT),
@@ -123,8 +125,8 @@ def tile_attend_beamvocab_kernel(tc, hid, voc_words, voc_scales, bonus, offs, ou
             at = WORD_BYTES * (c0 - first)
             nc.tensor.matmul_mx(
                 sums[:, :n],
-                lhsT=codes[:].bitcast(FP8X4),
-                lhsT_scale=plane[:],
+                lhsT=codes.bitcast(FP8X4),
+                lhsT_scale=plane,
                 rhs=row[:, at : at + WORD_BYTES * n].bitcast(FP4X4),
                 rhs_scale=voc_scale_sb[:, z, c0 : c0 + n],
                 start=(z == 0),
@@ -144,8 +146,8 @@ def tile_attend_beamvocab_kernel(tc, hid, voc_words, voc_scales, bonus, offs, ou
         for n in WARM_UPS:
             nc.tensor.matmul_mx(
                 early_sums[0][:, :n],
-                lhsT=hid_mx[0][0][:].bitcast(FP8X4),
-                lhsT_scale=hid_mx[0][1][:],
+                lhsT=hid_mx[0][0].bitcast(FP8X4),
+                lhsT_scale=hid_mx[0][1],
                 rhs=first_bytes[:, : WORD_BYTES * n].bitcast(FP4X4),
                 rhs_scale=first_bytes[:, :n],
                 start=True,

@@ -47,12 +47,12 @@ def tile_attend_beamvocab_kernel(tc, hid, voc_words, voc_scales, bonus, offs, ou
         psum = ctx.enter_context(tc.psum_pool(name="psum", bufs=1))
 
         def load_hid(z):
-            rows_sb = keep.tile([P, PACK, Q], F32, name="hid_rows%d" % z, align_bytes=256)
+            rows_sb = keep.tile([P, PACK, Q], F32, name="hid_rows%d" % z, align_bytes=1024)
             nc.sync.dma_start(rows_sb[:], hid[z * K_PASS : (z + 1) * K_PASS, :].rearrange("(p t) q -> p t q", t=PACK))
             return rows_sb
 
         def load_words(passes, first, width):
-            words_sb = keep.tile([P, len(passes), WORD_BYTES * width], U8, name="words%d_%d" % (passes[0], first), align_bytes=256)
+            words_sb = keep.tile([P, len(passes), WORD_BYTES * width], U8, name="words%d_%d" % (passes[0], first), align_bytes=1024)
             words_hbm = voc_words[passes[0] : passes[-1] + 1, :, WORD_BYTES * first : WORD_BYTES * (first + width)]
             nc.sync.dma_start(words_sb[:].bitcast(I32), words_hbm.bitcast(I32).rearrange("z p c -> p z c"))
             for k, z in enumerate(passes):
@@ -62,9 +62,9 @@ def tile_attend_beamvocab_kernel(tc, hid, voc_words, voc_scales, bonus, offs, ou
             load_words([z], sum(EARLY_PIECES[z][:k]), EARLY_PIECES[z][k])
 
         def quantise_hid(z, rows_sb):
-            grouped = keep.tile([P, Q, PACK], BF16, name="grouped%d" % z, align_bytes=256)
-            codes = keep.tile([P, CODES_AT + Q], U32, name="hid_codes%d" % z, align_bytes=256)[:, CODES_AT:]
-            plane = keep.tile([P, PLANE_AT + Q], U8, name="hid_plane%d" % z, align_bytes=256)[:, PLANE_AT:]
+            grouped = keep.tile([P, Q, PACK], BF16, name="grouped%d" % z, align_bytes=1024)
+            codes = keep.tile([P, CODES_AT + Q], U32, name="hid_codes%d" % z, align_bytes=1024)[:, CODES_AT:]
+            plane = keep.tile([P, PLANE_AT + Q], U8, name="hid_plane%d" % z, align_bytes=1024)[:, PLANE_AT:]
             for copy, c0, c1 in (
                 (nc.vector.tensor_copy, 0, HALF),
                 (nc.vector.tensor_copy, HALF, CAST_SPLIT),
@@ -87,14 +87,14 @@ def tile_attend_beamvocab_kernel(tc, hid, voc_words, voc_scales, bonus, offs, ou
         load_early(0, 0)
         load_early(0, 1)
 
-        voc_scale_sb = keep.tile([P, PASSES, V], U8, name="voc_plane", align_bytes=256)
+        voc_scale_sb = keep.tile([P, PASSES, V], U8, name="voc_plane", align_bytes=1024)
         scale_rows = voc_scales.bitcast(I32).rearrange("z (a r) c -> r a z c", r=SCALE_ROWS)
         for r in range(SCALE_ROWS):
             nc.sync.dma_start(voc_scale_sb[:].bitcast(I32)[r:P:QUADRANT, :, :], scale_rows[r])
-        offsets = keep.tile([P, I // GROUP_ROWS], U16, name="offsets", align_bytes=256)
+        offsets = keep.tile([P, I // GROUP_ROWS], U16, name="offsets", align_bytes=1024)
         nc.sync.dma_start(offsets[:], offs)
 
-        spread = keep.tile([P, V], F32, name="spread", align_bytes=256)
+        spread = keep.tile([P, V], F32, name="spread", align_bytes=1024)
         nc.vector.memset(spread[:], 0.0)
 
         hid_mx = [quantise_hid(0, first_rows)]
@@ -106,11 +106,11 @@ def tile_attend_beamvocab_kernel(tc, hid, voc_words, voc_scales, bonus, offs, ou
             load_early(1, k)
         for k, width in enumerate(LATE_PIECES):
             load_words(list(range(PASSES)), EARLY + sum(LATE_PIECES[:k]), width)
-        bonus_sb = keep.tile([P, I], F32, name="bonus_sb", align_bytes=256)
+        bonus_sb = keep.tile([P, I], F32, name="bonus_sb", align_bytes=1024)
         nc.sync.dma_start(bonus_sb[:], bonus)
         hid_mx.append(quantise_hid(1, second_rows))
 
-        logits = keep.tile([P, V], F32, name="logits", align_bytes=256)
+        logits = keep.tile([P, V], F32, name="logits", align_bytes=1024)
         widths = [GROUP] * (V // GROUP - 1) + [NARROW] * (GROUP // NARROW)
         starts = [sum(widths[:g]) for g in range(len(widths))]
         early_groups = EARLY // GROUP
@@ -164,18 +164,18 @@ def tile_attend_beamvocab_kernel(tc, hid, voc_words, voc_scales, bonus, offs, ou
                 one_pass(g, z, sums)
             copy_out(g, sums)
 
-        scores = keep.tile([P, I], F32, name="scores", align_bytes=256)
+        scores = keep.tile([P, I], F32, name="scores", align_bytes=1024)
         nc.vector.tensor_tensor(scores[:], logits[:].indirect(offsets[:]), bonus_sb[:], ALU.add)
 
         neg_max = keep.tile([P, 1], F32, name="neg_max")
         nc.vector.tensor_reduce(neg_max[:], scores[:], AX.X, ALU.max, negate=True)
-        exps = keep.tile([P, I], F32, name="exps", align_bytes=256)
+        exps = keep.tile([P, I], F32, name="exps", align_bytes=1024)
         total = keep.tile([P, 1], F32, name="total")
         nc.scalar.activation(exps[:], scores[:], ACT.Exp, bias=neg_max[:], accum_out=total[:])
 
         inv_total = keep.tile([P, 1], F32, name="inv_total")
         nc.vector.reciprocal(inv_total[:], total[:])
-        weights = keep.tile([P, I], F32, name="weights", align_bytes=256)
+        weights = keep.tile([P, I], F32, name="weights", align_bytes=1024)
         nc.vector.tensor_scalar(weights[:], exps[:], inv_total[:], float(I), ALU.mult, ALU.mult)
         nc.vector.tensor_copy(spread[:].indirect(offsets[:]), weights[:])
         nc.sync.dma_start(out, spread[:])

@@ -61,24 +61,20 @@ def tile_attend_beamvocab_kernel(tc, hid, voc_words, voc_scales, bonus, offs, ou
         def load_early(z, k):
             load_words([z], sum(EARLY_PIECES[z][:k]), EARLY_PIECES[z][k])
 
-        def quantise_hid(z, rows_sb):
+        def quantise_hid(z, rows_sb, shares, cuts):
             grouped = keep.tile([P, Q, PACK], BF16, name="grouped%d" % z, align_bytes=1024)
             codes = keep.tile([P, CODES_AT + Q], U32, name="hid_codes%d" % z, align_bytes=1024)[:, CODES_AT:]
             plane = keep.tile([P, PLANE_AT + Q], U8, name="hid_plane%d" % z, align_bytes=1024)[:, PLANE_AT:]
-            for copy, c0, c1 in (
-                (nc.vector.tensor_copy, 0, HALF),
-                (nc.vector.tensor_copy, HALF, CAST_SPLIT),
-                (nc.scalar.copy, CAST_SPLIT, Q),
-            ):
+            for copy, c0, c1 in shares:
                 copy(
                     grouped[:, c0:c1, :].rearrange("p (c i) t -> p c t i", i=LINE),
                     rows_sb[:, :, c0:c1].rearrange("p t (c i) -> p c t i", i=LINE),
                 )
-            for c0 in (0, HALF):
+            for c0, c1 in cuts:
                 nc.vector.quantize_mx(
-                    codes[:, c0 : c0 + HALF].bitcast(FP8X4),
-                    plane[:, c0 : c0 + HALF],
-                    grouped[:, c0 : c0 + HALF, :].rearrange("p q t -> p (q t)"),
+                    codes[:, c0:c1].bitcast(FP8X4),
+                    plane[:, c0:c1],
+                    grouped[:, c0:c1, :].rearrange("p q t -> p (q t)"),
                 )
             return (codes, plane)
 
@@ -97,7 +93,7 @@ def tile_attend_beamvocab_kernel(tc, hid, voc_words, voc_scales, bonus, offs, ou
         spread = keep.tile([P, V], F32, name="spread", align_bytes=1024)
         nc.vector.memset(spread[:], 0.0)
 
-        hid_mx = [quantise_hid(0, first_rows)]
+        hid_mx = [quantise_hid(0, first_rows, [(nc.vector.tensor_copy, 0, Q)], [(0, Q)])]
 
         load_early(0, 2)
         second_rows = load_hid(1)
@@ -108,7 +104,8 @@ def tile_attend_beamvocab_kernel(tc, hid, voc_words, voc_scales, bonus, offs, ou
             load_words(list(range(PASSES)), EARLY + sum(LATE_PIECES[:k]), width)
         bonus_sb = keep.tile([P, I], F32, name="bonus_sb", align_bytes=1024)
         nc.sync.dma_start(bonus_sb[:], bonus)
-        hid_mx.append(quantise_hid(1, second_rows))
+        shares = [(nc.vector.tensor_copy, 0, HALF), (nc.vector.tensor_copy, HALF, CAST_SPLIT), (nc.scalar.copy, CAST_SPLIT, Q)]
+        hid_mx.append(quantise_hid(1, second_rows, shares, [(0, HALF), (HALF, Q)]))
 
         logits = keep.tile([P, V], F32, name="logits", align_bytes=1024)
         widths = [GROUP] * (V // GROUP - 1) + [NARROW] * (GROUP // NARROW)

@@ -30,7 +30,7 @@ BANK = 512
 BANKS = 8
 GROUP = 256
 NARROW = 128
-EARLY_PIECES = ((256, 256, 512, 512), (768, 768))
+EARLY_PIECES = ((1024, 512), (512, 1024))
 EARLY = sum(EARLY_PIECES[0])
 LATE_PIECES = (512,)
 WARM_UPS = (256, 128)
@@ -81,29 +81,30 @@ def tile_attend_beamvocab_kernel(tc, hid, voc_words, voc_scales, bonus, offs, ou
         first_rows = load_hid(0)
         word_rows = [[] for z in range(PASSES)]
         load_early(0, 0)
-        load_early(0, 1)
 
         voc_scale_sb = keep.tile([P, PASSES, V], U8, name="voc_plane", align_bytes=1024)
         scale_rows = voc_scales.bitcast(I32).rearrange("z (a r) c -> r a z c", r=SCALE_ROWS)
-        for r in range(SCALE_ROWS):
-            nc.sync.dma_start(voc_scale_sb[:].bitcast(I32)[r:P:QUADRANT, :, :], scale_rows[r])
-        offsets = keep.tile([P, I // GROUP_ROWS], U16, name="offsets", align_bytes=1024)
-        nc.sync.dma_start(offsets[:], offs)
+        plane_words = voc_scale_sb[:].bitcast(I32)
+        nc.sync.dma_start(plane_words[0:P:QUADRANT, :, :], scale_rows[0])
+        for z in range(PASSES):
+            for r in range(1, SCALE_ROWS):
+                nc.sync.dma_start(plane_words[r:P:QUADRANT, z, :], scale_rows[r, :, z, :])
 
         spread = keep.tile([P, V], F32, name="spread", align_bytes=1024)
         nc.vector.memset(spread[:], 0.0)
 
         hid_mx = [quantise_hid(0, first_rows, [(nc.vector.tensor_copy, 0, Q)], [(0, Q)])]
 
-        load_early(0, 2)
         second_rows = load_hid(1)
-        load_early(0, 3)
+        load_early(0, 1)
         for k in range(len(EARLY_PIECES[1])):
             load_early(1, k)
         for k, width in enumerate(LATE_PIECES):
             load_words(list(range(PASSES)), EARLY + sum(LATE_PIECES[:k]), width)
         bonus_sb = keep.tile([P, I], F32, name="bonus_sb", align_bytes=1024)
         nc.sync.dma_start(bonus_sb[:], bonus)
+        offsets = keep.tile([P, I // GROUP_ROWS], U16, name="offsets", align_bytes=1024)
+        nc.sync.dma_start(offsets[:], offs)
         shares = [(nc.vector.tensor_copy, 0, HALF), (nc.vector.tensor_copy, HALF, CAST_SPLIT), (nc.scalar.copy, CAST_SPLIT, Q)]
         hid_mx.append(quantise_hid(1, second_rows, shares, [(0, HALF), (HALF, Q)]))
 

@@ -26,6 +26,7 @@ LINE = 4
 GROUP_ROWS = 16
 QUADRANT = 32
 SCALE_ROWS = 4
+SPLIT_ROWS = 2
 BANK = 512
 BANKS = 8
 GROUP = 256
@@ -85,10 +86,12 @@ def tile_attend_beamvocab_kernel(tc, hid, voc_words, voc_scales, bonus, offs, ou
         voc_scale_sb = keep.tile([P, PASSES, V], U8, name="voc_plane", align_bytes=1024)
         scale_rows = voc_scales.bitcast(I32).rearrange("z (a r) c -> r a z c", r=SCALE_ROWS)
         plane_words = voc_scale_sb[:].bitcast(I32)
-        nc.sync.dma_start(plane_words[0:P:QUADRANT, :, :], scale_rows[0])
-        for z in range(PASSES):
-            for r in range(1, SCALE_ROWS):
-                nc.sync.dma_start(plane_words[r:P:QUADRANT, z, :], scale_rows[r, :, z, :])
+        for r in range(SPLIT_ROWS):
+            nc.sync.dma_start(plane_words[r:P:QUADRANT, 0, :], scale_rows[r, :, 0, :])
+        for r in range(SPLIT_ROWS, SCALE_ROWS):
+            nc.sync.dma_start(plane_words[r:P:QUADRANT, :, :], scale_rows[r])
+        for r in range(SPLIT_ROWS):
+            nc.sync.dma_start(plane_words[r:P:QUADRANT, 1, :], scale_rows[r, :, 1, :])
 
         spread = keep.tile([P, V], F32, name="spread", align_bytes=1024)
         nc.vector.memset(spread[:], 0.0)

@@ -34,7 +34,6 @@ NARROW = 128
 EARLY_PIECES = ((1024, 512), (512, 1024))
 EARLY = sum(EARLY_PIECES[0])
 LATE_PIECES = (512,)
-WARM_UPS = (256, 128)
 CAST_SPLIT = 96
 HALF = Q // 2
 CODES_AT = 32
@@ -143,17 +142,6 @@ def tile_attend_beamvocab_kernel(tc, hid, voc_words, voc_scales, bonus, offs, ou
 
         early_sums = [open_group(g) for g in range(early_groups)]
 
-        first_bytes = word_rows[0][0][2]
-        for n in WARM_UPS:
-            nc.tensor.matmul_mx(
-                early_sums[0][:, :n],
-                lhsT=hid_mx[0][0].bitcast(FP8X4),
-                lhsT_scale=hid_mx[0][1],
-                rhs=first_bytes[:, : WORD_BYTES * n].bitcast(FP4X4),
-                rhs_scale=first_bytes[:, :n],
-                start=True,
-                stop=True,
-            )
         for z in range(PASSES):
             for g in range(early_groups):
                 one_pass(g, z, early_sums[g])

from contextlib import ExitStack

import concourse.mybir as mybir

D, V, Q, I = 1024, 2048, 128, 512
FLOPS = 2 * D * V * Q

F32 = mybir.dt.float32
BF16 = mybir.dt.bfloat16
I32 = mybir.dt.int32
U32 = mybir.dt.uint32
U16 = mybir.dt.uint16
U8 = mybir.dt.uint8
FP8X4 = mybir.dt.float8_e4m3fn_x4
FP4X4 = mybir.dt.float4_e2m1fn_x4
ALU = mybir.AluOpType
ACT = mybir.ActivationFunctionType
AX = mybir.AxisListType

P = 128
PACK = 4
K_PASS = P * PACK
PASSES = D // K_PASS
WORD_BYTES = 2
LINE = 4
GROUP_ROWS = 16
QUADRANT = 32
SCALE_ROWS = 4
SPLIT_ROWS = 2
BANK = 512
BANKS = 8
GROUP = 256
NARROW = 128
EARLY_PIECES = ((1024, 512), (512, 1024))
EARLY = sum(EARLY_PIECES[0])
LATE_PIECES = (512,)
CAST_SPLIT = 96
HALF = Q // 2
CODES_AT = 32
PLANE_AT = 64


def tile_attend_beamvocab_kernel(tc, hid, voc_words, voc_scales, bonus, offs, out):
    nc = tc.nc
    with ExitStack() as ctx:
        keep = ctx.enter_context(tc.tile_pool(name="keep", bufs=1))
        psum = ctx.enter_context(tc.psum_pool(name="psum", bufs=1))

        def load_hid(z):
            rows_sb = keep.tile([P, PACK, Q], F32, name="hid_rows%d" % z, align_bytes=1024)
            nc.sync.dma_start(rows_sb[:], hid[z * K_PASS : (z + 1) * K_PASS, :].rearrange("(p t) q -> p t q", t=PACK))
            return rows_sb

        def load_words(passes, first, width):
            words_sb = keep.tile([P, len(passes), WORD_BYTES * width], U8, name="words%d_%d" % (passes[0], first), align_bytes=1024)
            words_hbm = voc_words[passes[0] : passes[-1] + 1, :, WORD_BYTES * first : WORD_BYTES * (first + width)]
            nc.sync.dma_start(words_sb[:].bitcast(I32), words_hbm.bitcast(I32).rearrange("z p c -> p z c"))
            for k, z in enumerate(passes):
                word_rows[z].append((first, width, words_sb[:, k, :]))

        def load_early(z, k):
            load_words([z], sum(EARLY_PIECES[z][:k]), EARLY_PIECES[z][k])

        def quantise_hid(z, rows_sb, shares, cuts):
            grouped = keep.tile([P, Q, PACK], BF16, name="grouped%d" % z, align_bytes=1024)
            codes = keep.tile([P, CODES_AT + Q], U32, name="hid_codes%d" % z, align_bytes=1024)[:, CODES_AT:]
            plane = keep.tile([P, PLANE_AT + Q], U8, name="hid_plane%d" % z, align_bytes=1024)[:, PLANE_AT:]
            for copy, c0, c1 in shares:
                copy(
                    grouped[:, c0:c1, :].rearrange("p (c i) t -> p c t i", i=LINE),
                    rows_sb[:, :, c0:c1].rearrange("p t (c i) -> p c t i", i=LINE),
                )
            for c0, c1 in cuts:
                nc.vector.quantize_mx(
                    codes[:, c0:c1].bitcast(FP8X4),
                    plane[:, c0:c1],
                    grouped[:, c0:c1, :].rearrange("p q t -> p (q t)"),
                )
            return (codes, plane)

        first_rows = load_hid(0)
        word_rows = [[] for z in range(PASSES)]
        load_early(0, 0)

        voc_scale_sb = keep.tile([P, PASSES, V], U8, name="voc_plane", align_bytes=1024)
        scale_rows = voc_scales.bitcast(I32).rearrange("z (a r) c -> r a z c", r=SCALE_ROWS)
        plane_words = voc_scale_sb[:].bitcast(I32)
        for r in range(SPLIT_ROWS):
            nc.sync.dma_start(plane_words[r:P:QUADRANT, 0, :], scale_rows[r, :, 0, :])
        for r in range(SPLIT_ROWS, SCALE_ROWS):
            nc.sync.dma_start(plane_words[r:P:QUADRANT, :, :], scale_rows[r])
        for r in range(SPLIT_ROWS):
            nc.sync.dma_start(plane_words[r:P:QUADRANT, 1, :], scale_rows[r, :, 1, :])

        spread = keep.tile([P, V], F32, name="spread", align_bytes=1024)
        nc.vector.memset(spread[:], 0.0)

        hid_mx = [quantise_hid(0, first_rows, [(nc.vector.tensor_copy, 0, Q)], [(0, Q)])]

        second_rows = load_hid(1)
        load_early(0, 1)
        for k in range(len(EARLY_PIECES[1])):
            load_early(1, k)
        for k, width in enumerate(LATE_PIECES):
            load_words(list(range(PASSES)), EARLY + sum(LATE_PIECES[:k]), width)
        bonus_sb = keep.tile([P, I], F32, name="bonus_sb", align_bytes=1024)
        nc.sync.dma_start(bonus_sb[:], bonus)
        offsets = keep.tile([P, I // GROUP_ROWS], U16, name="offsets", align_bytes=1024)
        nc.sync.dma_start(offsets[:], offs)
        shares = [(nc.vector.tensor_copy, 0, HALF), (nc.vector.tensor_copy, HALF, CAST_SPLIT), (nc.scalar.copy, CAST_SPLIT, Q)]
        hid_mx.append(quantise_hid(1, second_rows, shares, [(0, HALF), (HALF, Q)]))

        logits = keep.tile([P, V], F32, name="logits", align_bytes=1024)
        widths = [GROUP] * (V // GROUP - 1) + [NARROW] * (GROUP // NARROW)
        starts = [sum(widths[:g]) for g in range(len(widths))]
        early_groups = EARLY // GROUP

        def open_group(g):
            return psum.tile([P, BANK], F32, name="sums%d" % g, tag="bank%d" % (g % BANKS))

        def one_pass(g, z, sums):
            c0, n = starts[g], widths[g]
            codes, plane = hid_mx[z]
            first, row = [(f, r) for f, width, r in word_rows[z] if f <= c0 < f + width][0]
            at = WORD_BYTES * (c0 - first)
            nc.tensor.matmul_mx(
                sums[:, :n],
                lhsT=codes.bitcast(FP8X4),
                lhsT_scale=plane,
                rhs=row[:, at : at + WORD_BYTES * n].bitcast(FP4X4),
                rhs_scale=voc_scale_sb[:, z, c0 : c0 + n],
                start=(z == 0),
                stop=(z == PASSES - 1),
            )

        def copy_out(g, sums):
            c0, n = starts[g], widths[g]
            if (len(widths) - g) % 2 == 1:
                nc.scalar.activation(logits[:, c0 : c0 + n], sums[:, :n], ACT.Copy)
            else:
                nc.vector.tensor_copy(logits[:, c0 : c0 + n], sums[:, :n])

        early_sums = [open_group(g) for g in range(early_groups)]

        for z in range(PASSES):
            for g in range(early_groups):
                one_pass(g, z, early_sums[g])
        for g in range(early_groups):
            copy_out(g, early_sums[g])
        for g in range(early_groups, len(widths)):
            sums = open_group(g)
            for z in range(PASSES):
                one_pass(g, z, sums)
            copy_out(g, sums)

        scores = keep.tile([P, I], F32, name="scores", align_bytes=1024)
        nc.vector.tensor_tensor(scores[:], logits[:].indirect(offsets[:]), bonus_sb[:], ALU.add)

        neg_max = keep.tile([P, 1], F32, name="neg_max")
        nc.vector.tensor_reduce(neg_max[:], scores[:], AX.X, ALU.max, negate=True)
        exps = keep.tile([P, I], F32, name="exps", align_bytes=1024)
        total = keep.tile([P, 1], F32, name="total")
        nc.scalar.activation(exps[:], scores[:], ACT.Exp, bias=neg_max[:], accum_out=total[:])

        inv_total = keep.tile([P, 1], F32, name="inv_total")
        nc.vector.reciprocal(inv_total[:], total[:])
        weights = keep.tile([P, I], F32, name="weights", align_bytes=1024)
        nc.vector.tensor_scalar(weights[:], exps[:], inv_total[:], float(I), ALU.mult, ALU.mult)
        nc.vector.tensor_copy(spread[:].indirect(offsets[:]), weights[:])
        nc.sync.dma_start(out, spread[:])
